import numpy as np, ml_dtypes
CORES = [23,119,17,113]
N = 4
import mx_ref
BF = ml_dtypes.bfloat16
def pick(q, e):
    c = np.concatenate([q[0].reshape(128, -1, 4), np.zeros((128, 1, 4), np.uint8)], axis=1); s = np.concatenate([q[1], np.ones((16, 1), np.uint8)], axis=1)
    return (np.ascontiguousarray(c[:, e].reshape(128, -1)), np.ascontiguousarray(s[:, e]))
def join(*qs):
    return (np.concatenate([q[0] for q in qs], axis=1), np.concatenate([q[1] for q in qs], axis=1))
def put(q, e, v):
    c, s = q[0].reshape(128, -1, 4).copy(), q[1].copy(); c[:, e] = v[0].reshape(128, -1, 4); s[:, e] = v[1]
    return (c.reshape(128, -1), s)
def pk(c, s):
    return (np.ascontiguousarray(c), mx_ref.live(s))
def emit(q):
    return q[0], q[1]
def decode(q):
    o = []
    for b in range(4):
        e = np.zeros((128, 128, 4), np.float32); e[np.arange(128), np.arange(128), b] = 1
        o.append(mx_ref.matmul(mx_ref.quantize(e.reshape(128, 512).astype(BF)), q))
    return np.stack(o, axis=2).reshape(128, -1)
def cut(t, i, w=512):
    return t[:, w * i:w * i + w]
def f(rng, *shape):
    return mx_ref.flush((rng.standard_normal(shape, dtype=np.float32) * np.exp2(rng.integers(-2, 3, shape[:-1] + (1,)))).astype(BF))
def wide(rng, *shape, cols=0):
    v = rng.standard_normal(shape, dtype=np.float32) * np.exp2(rng.integers(-12, 13, shape)).astype(np.float32)
    if cols: v *= np.repeat(np.exp2(rng.integers(-cols, cols + 1, shape[:-2] + (1, shape[-1] // 4))) * (rng.random(shape[:-2] + (1, shape[-1] // 4)) > 0.0625), 4, axis=-1).astype(np.float32)
    return mx_ref.flush(v.astype(BF))
T, L, O, LV, V, F = 16, 16, 3, 2, 192, 64
DI, DJ = np.array([1, 1, 0, 0]), np.array([1, 0, 1, 0])
def align(g):
    n = g.shape[0]
    p, back = np.zeros((n, L, L), np.float32), np.full((n, L, L), 3)
    for i in range(L):
        for j in range(L):
            if i == 0 and j == 0:
                p[:, i, j] = g[:, i, j]
                continue
            if i == 0: best, back[:, i, j] = p[:, i, j - 1], 2
            elif j == 0: best, back[:, i, j] = p[:, i - 1, j], 1
            else:
                c = np.stack([p[:, i - 1, j - 1], p[:, i - 1, j], p[:, i, j - 1]])
                best, back[:, i, j] = np.max(c, axis=0), np.argmax(c, axis=0)
            p[:, i, j] = g[:, i, j] + best
    m, i, j, low = np.arange(n), np.full(n, L - 1), np.full(n, L - 1), np.zeros((n, L), int)
    for s in range(2 * L - 1):
        low[m, i] = j
        k = back[m, i, j]
        i, j = i - DI[k], j - DJ[k]
    return low
def clear(v):
    v = v.astype(np.float32)
    v[np.abs(v) < np.float32(2.0 ** -14)] = 0
    return v.astype(BF)
def lay(v):
    return np.ascontiguousarray(v.transpose(0, 3, 1, 2, 4)).reshape(N, 128, 4 * T * L).astype(np.float32).astype(BF)
def setup_inputs(rng):
    return {"x": clear(f(rng, N, 128, 4 * T * L)), "w": f(rng, N, 128, 512 * O)}
def setup_inputs_ties(rng):
    kind = (np.arange(T) // N) % 3
    u = rng.choice([-1.0, 1.0], (T, 128, 4)) * np.exp2(rng.integers(-3, 4, (T, 1, 1)))
    s = rng.integers(-1, 2, (N, T, L)).astype(np.float64)
    m = rng.choice([-1.0, 1.0], (N, T, L))
    s[:, :, 0] = 1
    m[:, :, 0] = 1
    m[1::2] = 0
    s[:, kind == 0] = 1
    s[:, kind == 1] = m[:, kind == 1]
    return {"x": lay(s[:, :, :, None, None] * u[None, :, None]), "w": f(rng, N, 128, 512 * O)}
def setup_inputs_near(rng):
    kind = (np.arange(T) // N) % 3
    even, one = kind != 1, kind == 1
    u = rng.choice([-1.0, 1.0], (T, 1, 128, 4))
    v = np.zeros((N, T, L, 128, 4))
    v[:, even, :, :120] = u[even][:, :, :120]
    for r in range(N):
        v[r][one, 0, :64] = 4 * u[one][:, 0, :64]
        v[r][one, 1:, 64 + 6 * r:70 + 6 * r] = rng.choice([-1.0, 1.0], (int(np.count_nonzero(one)), L - 1, 6, 4))
    a = rng.integers(1, 4, (N, T, L)) * rng.choice([-1.0, 1.0], (N, T, L))
    a[:, kind == 2] = 1
    a[0::2][:, kind == 2, L - 1] = 3
    a[1::2][:, kind == 2, 0] = 3
    v[:, :, :, 127, 0] = a * np.where(one, 2.0 ** -6, 2.0 ** -5)[None, :, None]
    return {"x": lay(v * np.exp2(rng.integers(-3, 4, (1, T, 1, 1, 1)))), "w": f(rng, N, 128, 512 * O)}
def setup_inputs_far(rng):
    kind = (np.arange(T) // N) % 3
    deep, side = kind == 2, np.arange(T) // 2 % 2 == 1
    v = 1.5 + 0.5 * rng.random((N, T, L, 128, 4))
    v[:, deep] = 1
    ones = np.array([bin(k).count("1") for k in range(N)])
    c = ones[np.arange(N)[:, None] ^ rng.integers(0, N, T)[None, :]]
    e = -rng.integers(3, 9, (N, T, L))
    e[:, :, 0] = 0
    low = np.exp2(29.0 - c[:, :, None] + e) * (1 - 2 * (c % 2))[:, :, None]
    mixed = np.exp2(rng.integers(20, 30, (N, T, L))) * rng.choice([-1.0, 1.0], (N, T, L))
    mixed[:, :, 0] = 2.0 ** 29
    s = np.where((kind == 0)[None, :, None], low, mixed)
    s[0::2][:, deep] = 2.0 ** 30
    s[1::2][:, deep] = -2.0 ** 30
    s[0::2][:, deep & ~side, L - 1] = 2.0 ** 20
    s[1::2][:, deep & side, L - 1] = -2.0 ** 20
    return {"x": lay(v * s[:, :, :, None, None]), "w": f(rng, N, 128, 512 * O)}
def setup_inputs_warp(rng):
    p = rng.standard_normal((T, L, 128, 4)) * np.exp2(rng.integers(-2, 3, (T, 1, 128, 1)))
    i = np.sort(rng.integers(0, L, (N, T, L)), axis=2)
    v = p[np.arange(T)[None, :, None], i] + 0.25 * rng.standard_normal((N, T, L, 128, 4))
    return {"x": clear(lay(v)), "w": f(rng, N, 128, 512 * O)}
def setup_inputs_spread(rng):
    return {"x": clear(wide(rng, N, 128, 4 * T * L, cols=6)), "w": f(rng, N, 128, 512 * O)}
def check_inputs(d):
    b = []
    for k, least in (("x", 2.0 ** -14), ("w", 2.0 ** -30)):
        v = np.abs(d[k].astype(np.float32))
        if not (np.isfinite(v).all() and ((v == 0) | (v >= least) & (v <= 2.0 ** 30)).all()): b.append("a value of " + k)
    return b
def reference(x, w):
    y, pt = np.zeros((N, 128, O * V), np.float32), np.zeros((N, 1, V), np.float32)
    oc, osc = np.zeros((N, 128, 4 * F), np.uint8), np.zeros((N, 16, F), np.uint8)
    wq = [[mx_ref.quantize(np.ascontiguousarray(cut(w[r], o))) for o in range(O)] for r in range(N)]
    held = [mx_ref.quantize(np.ascontiguousarray(x[r])) for r in range(N)]
    at = 0
    for b in range(LV):
        n = T >> (b + 1)
        h = n * L
        new = []
        for r in range(N):
            p = r ^ (1 << b)
            k = np.arange((r >> b) & 1, T >> b, 2)
            e = (k[:, None] * L + np.arange(L)).reshape(-1)
            lower, upper = pick(held[min(r, p)], e), pick(held[max(r, p)], e)
            g = mx_ref.matmul(pick(lower, np.concatenate([np.arange(h), np.full(128 - h, -1)])), upper)[:h].reshape(n, L, n, L)
            j = align(g[np.arange(n), :, np.arange(n), :])
            met = pick(upper, (np.arange(n)[:, None] * L + j).reshape(-1))
            v = decode(join(lower, met))
            m = mx_ref.quantize(np.ascontiguousarray(((v[:, :4 * h] + v[:, 4 * h:]) * np.float32(0.5)).astype(BF)))
            pt[r, 0, at:at + h] = j.reshape(-1)
            for o in range(O): y[r, :, o * V + at:o * V + at + h] = mx_ref.matmul(wq[r][o], m)
            new.append(m)
        held = new
        at += h
    for r in range(N): oc[r], osc[r] = emit(held[r])
    return {"y": y, "pt": pt, "oc": oc, "osc": osc}

@@ -1,0 +1,389 @@
+from concourse.bass import DstId, RemoteDMATransfer
+from concourse.mybir import dt, AluOpType, ActivationFunctionType
+
+ALU = AluOpType
+AF = ActivationFunctionType
+X4, U8, F32, BF = "float8_e4m3fn_x4", "uint8", "float32", "bfloat16"
+LOW = -1e29
+
+SCRATCH = {
+    "xin": ("sbuf", [128, 4, 4, 64], BF),
+    "xt": ("sbuf", [128, 1024], BF),
+    "snd": ("sbuf", [128, 128], X4), "snds": ("sbuf", [128, 128], U8),
+    "lnd": ("sbuf", [128, 512], X4), "lnds": ("sbuf", [128, 512], U8),
+    "win": ("sbuf", [128, 1536], BF),
+    "wq": ("sbuf", [128, 384], X4), "wqs": ("sbuf", [128, 384], U8),
+    "ones": ("sbuf", [128, 128], BF), "ident": ("sbuf", [128, 128], BF),
+    "et": ("sbuf", [128, 1032], BF),
+    "eq": ("sbuf", [128, 512], X4), "eqs": ("sbuf", [128, 512], U8),
+    "bas": ("sbuf", [128, 32], F32), "bt": ("sbuf", [128, 32], F32),
+    "nb": ("sbuf", [128, 1], F32), "pb": ("sbuf", [128, 1], F32),
+    "dn": ("sbuf", [128, 17], F32),
+    "sen": ("sbuf", [128, 2], BF), "rs": ("sbuf", [128, 136], BF),
+    "spr": ("sbuf", [128, 512], F32),
+    "gr": ("sbuf", [128, 128], F32),
+    "dp": ("sbuf", [128, 4, 17], F32),
+    "um": ("sbuf", [128, 4, 16], F32),
+    "dg": ("sbuf", [128, 64], BF), "mk": ("sbuf", [128, 128], BF),
+    "tb": ("sbuf", [128, 170], BF), "ab": ("sbuf", [128, 136], BF),
+    "en": ("sbuf", [128, 68], F32), "sm": ("sbuf", [128, 1088], F32),
+    "jt": ("sbuf", [128, 32], F32),
+    "off0": ("sbuf", [128, 12], "uint16"), "off1": ("sbuf", [128, 4], "uint16"),
+    "pj0": ("sbuf", [128, 16], F32), "pj1": ("sbuf", [128, 16], F32),
+    "pk0": ("sbuf", [128, 128], X4), "pk0s": ("sbuf", [128, 128], U8),
+    "pkl": ("sbuf", [128, 192], X4), "pkls": ("sbuf", [128, 192], U8),
+    "pk1": ("sbuf", [128, 320], X4), "pk1s": ("sbuf", [128, 320], U8),
+    "t0": ("sbuf", [128, 576], BF), "tl": ("sbuf", [128, 512], BF), "t1": ("sbuf", [128, 512], BF),
+    "q0": ("sbuf", [128, 144], X4), "q0s": ("sbuf", [128, 144], U8),
+    "ql": ("sbuf", [128, 128], X4), "qls": ("sbuf", [128, 128], U8),
+    "q1": ("sbuf", [128, 128], X4), "q1s": ("sbuf", [128, 128], U8),
+    "ys0": ("sbuf", [128, 3, 8, 16], F32), "ys1": ("sbuf", [128, 192], F32),
+}
+for _k in range(8):
+    SCRATCH["ps%d" % _k] = ("psum", [128, 512], F32)
+
+NSEM, POOL = 140, 8
+SEMAPHORES = ["arrp", "arro", "sent"] + ["s%d" % _k for _k in range(NSEM)]
+
+
+def _emit(ops, queues, T):
+    n = len(ops)
+    members = {}
+    for i, o in enumerate(ops):
+        if o["grp"]:
+            members.setdefault(o["grp"], []).append(i)
+    known = {q: set() for q in queues}
+    before = [None] * n
+    waiters = {}
+    for i, o in enumerate(ops):
+        k = known[o["q"]]
+        w = []
+        ext = [d for d in o["deps"] if isinstance(d, tuple)]
+        own = sorted(set(d for d in o["deps"] if not isinstance(d, tuple)), reverse=True)
+        for d in ext:
+            if d not in k:
+                k.add(d)
+                w.append(d)
+        for d in own:
+            if d in k:
+                continue
+            for m in (members[ops[d]["grp"]] if ops[d]["grp"] else [d]):
+                k.add(m)
+                k |= before[m]
+            w.append(d)
+            waiters.setdefault(ops[d]["grp"] or d, set()).add(o["q"])
+        o["waits"] = w
+        before[i] = set(k)
+    nxt = [0]
+
+    def fresh():
+        nxt[0] += 1
+        return "s%d" % (nxt[0] - 1)
+
+    pools = {q: [] for q in queues}
+    turn = {q: 0 for q in queues}
+    sem, total = {}, {}
+    for i, o in enumerate(ops):
+        key = o["grp"] or i
+        if key in waiters and key not in sem:
+            if not o["grp"] and o["inc"] == 1 and waiters[key] == {o["q"]}:
+                p = pools[o["q"]]
+                if len(p) < POOL:
+                    p.append(fresh())
+                sem[key] = p[turn[o["q"]] % POOL]
+                turn[o["q"]] += 1
+            else:
+                sem[key] = fresh()
+                total[key] = sum(ops[m]["inc"] for m in members[key]) if o["grp"] else o["inc"]
+    count = {}
+    for i, o in enumerate(ops):
+        e = queues[o["q"]]
+        for d in o["waits"]:
+            if isinstance(d, tuple):
+                e.wait_ge(T.sem[d[0]], d[1])
+            else:
+                key = ops[d]["grp"] or d
+                e.wait_ge(T.sem[sem[key]], total[key] if key in total else count[sem[key]])
+        if o["fn"] is None:
+            continue
+        ins = o["fn"]()
+        key = o["grp"] or i
+        if key in sem:
+            ins.then_inc(T.sem[sem[key]], o["inc"])
+            count[sem[key]] = count.get(sem[key], 0) + o["inc"]
+
+
+def rank_program(g, core, T, topo):
+    r = T.rank_of(core)
+    if r is None:
+        return
+    V, S, P, Y = g.vector, g.scalar, g.tensor, g.sync
+    ops = []
+
+    def flat(ds):
+        out = []
+        for d in ds:
+            if isinstance(d, list):
+                out += flat(d)
+            else:
+                out.append(d)
+        return out
+
+    def op(q, fn, *deps, grp=None, inc=1):
+        ops.append({"q": q, "fn": fn, "deps": flat(deps), "grp": grp, "inc": inc})
+        return len(ops) - 1
+
+    def dma(q, out, in_, *deps, grp=None):
+        e = {"g": g, "y": Y, "s": S}[q]
+        return op(q, lambda: e.dma_start(out, in_), *deps, grp=grp, inc=16)
+
+    def fill(ap, c, *deps, grp=None):
+        return op("v", lambda: V.memset(ap, c), *deps, grp=grp)
+
+    def cp(q, out, in_, *deps, grp=None):
+        if q == "v":
+            return op("v", lambda: V.tensor_copy(out, in_), *deps, grp=grp)
+        return op("s", lambda: S.activation(out, in_, AF.Copy), *deps, grp=grp)
+
+    def quant(out, sc, in_, *deps, grp=None):
+        return op("v", lambda: V.quantize_mx(out, sc, in_), *deps, grp=grp)
+
+    def mm(bank, n, w, ws, a, x, xs, b, start, stop, *deps):
+        return op("p", lambda: P.matmul_mx(T["ps%d" % bank][:, 0:n], w[:, a:a + 128], ws[:, a:a + 128],
+                                           x[:, b:b + n], xs[:, b:b + n], start, stop), *deps)
+
+    def tt(out, a, b, o, *deps):
+        return op("v", lambda: V.tensor_tensor(out, a, b, o), *deps)
+
+    def scan(out, a, b, init, o0, o1, *deps):
+        return op("v", lambda: V.tensor_tensor_scan(out, a, b, init, o0, o1), *deps)
+
+    def quarter(a):
+        return slice(32 * a, 32 * a + 32)
+
+    BX, BO, AO, AX = 64, 128, 256, 384
+    even = r % 2 == 0
+    own = AO if even else BO
+    ab, bb = (0, 64) if r < 2 else (64, 0)
+
+    ldx = dma("y", T.xin[:], T.x[:])
+    f_ones = fill(T.ones[:], 1.0)
+    f_et = fill(T.et[:], 0.0)
+    f_t1 = fill(T.t1[:], 0.0)
+    f_tb = fill(T.tb[:], 0.0)
+    f_ab = fill(T.ab[:], 0.0)
+    f_rs = fill(T.rs[:], 1.0)
+    fill(T.mk[:], 1.0, grp="st")
+    ident = op("g", lambda: g.affine_select(T.ident[:], T.ones[:], [[-1, 128]], ALU.is_equal, 0.0, 0, 1), f_ones, grp="gs")
+    op("g", lambda: g.iota(T.bas[:], [[-64, 8], [16, 4]], 128, 0, allow_small_or_imprecise_dtypes=True), grp="gs")
+    op("g", lambda: g.iota(T.dn[:], [[-1, 17]], 16, 0, allow_small_or_imprecise_dtypes=True), grp="gs")
+
+    order = [r ^ 3, r ^ 1, r ^ 2, r] if even else [r ^ 1, r ^ 3, r, r ^ 2]
+    cx = [cp("v" if k < 2 else "s", T.xt[:, 256 * k:256 * k + 256], T.xin[:, :, order[k], :], ldx) for k in range(4)]
+    q_s = quant(T.snd[:], T.snds[:], T.xt[:, 0:512], cx[0], cx[1])
+    q_o = quant(T.lnd[:, own:own + 128], T.lnds[:, own:own + 128], T.xt[:, 512:1024], cx[2], cx[3])
+
+    def u8(v):
+        return v.bitcast(dt.uint8)
+
+    def bits(es):
+        return sum(1 << e for e in es)
+
+    peer = {k: T.cores[r ^ k] for k in (1, 2, 3)}
+    e1, e3 = topo.engines(core, peer[1]), topo.engines(core, peer[3])
+    far = [e for e in e1 if e in e3][:8]
+    near = [e for e in topo.engines(core, peer[2]) if e not in far][::2][:4]
+
+    def xfer(k, es, sem, src, dst):
+        a = topo.addr(peer[k])
+        return RemoteDMATransfer(dst_ids=[DstId(rid=a[0], pnc=a[1])], dma_engine_mask=bits(es), remote_sem=T.sem[sem], src=src, dst=dst)
+
+    h = 0 if even else 64
+    dc = AX if even else BX
+    dsc = dc - h
+    a1 = topo.addr(peer[1])
+    op("g", lambda: g.remote_dma(u8(T.lnd[:, own:own + 128]), u8(T.snd[:]), T.sem.arrp, T.sem.sent, a1[1], a1[0], bits(far)), q_s)
+    op("g", lambda: g.remote_dma_fused([
+        xfer(1, far[:4], "arrp", T.snds[:], T.lnds[:, own:own + 128]),
+        xfer(3, far[4:], "arro", T.snds[:], T.lnds[:, dsc:dsc + 128]),
+        xfer(2, near, "arro", T.lnds[:, own:own + 128], T.lnds[:, dsc:dsc + 128])], local_sem=T.sem.sent), q_o)
+    op("g", lambda: g.remote_dma_fused([
+        xfer(3, far, "arro", u8(T.snd[:, h:h + 64]), u8(T.lnd[:, dc:dc + 64])),
+        xfer(2, near, "arro", u8(T.lnd[:, own + h:own + h + 64]), u8(T.lnd[:, dc:dc + 64]))], local_sem=T.sem.sent))
+    ARRP, ARRO, SENT = ("arrp", 12), ("arro", 20), ("sent", 32)
+    ldw = dma("g", T.win[:], T.w[:], SENT)
+
+    st = fill(T.spr[0:32, :], 0.0, grp="st")
+    t_b = op("v", lambda: V.transpose(T.bt[:], T.bas[:]), ident)
+    ce = [cp("v", T.et[:, 517 * k + 2:517 * k + 514:4], T.ident[:], ident, f_et) for k in range(2)]
+    fill(T.dp[:, :, 0], LOW, grp="st")
+    fill(T.um[0:32, 0, 1:16], LOW, grp="st")
+    fill(T.um[0:32, 0, 0:1], 0.0, grp="st")
+    fill(T.sen[0:96, :], 17.0, grp="st")
+    fill(T.sen[96:128, :], 1.0, grp="st")
+    fill(T.rs[:, 0:136:34], 0.0, f_rs, grp="st")
+    fill(T.tb[0:96, 1:136:34], 17.0, f_tb, grp="st")
+    fill(T.tb[96:128, 1:136:34], 1.0, f_tb, grp="st")
+    cp("v", T.tb[0:96, 137:170:2], T.dn[0:96, :], f_tb, grp="st")
+    op("v", lambda: V.tensor_scalar(T.ab[:, 1:136:34], T.bt[:, 0:4], -1.0, -16.0, ALU.mult, ALU.add), t_b, f_ab, grp="st")
+    op("v", lambda: V.tensor_scalar(T.nb[:], T.bt[:, 0:1], -1.0, None, ALU.mult), t_b, grp="st")
+    op("v", lambda: V.tensor_scalar(T.pb[:], T.bt[:, 0:1], 16.0, None, ALU.add), t_b, grp="st")
+    cp("v", T.sm[0:32, 33:1088:544], T.bt[0:32, 0:2], t_b, grp="st")
+    q_e = []
+    for b in range(4):
+        k = 516 * (b % 2) + 2 - 2 * (b // 2)
+        q_e.append(quant(T.eq[:, 128 * b:128 * b + 128], T.eqs[:, 128 * b:128 * b + 128], T.et[:, k:k + 512], ce, grp="z"))
+    z1 = 0 if ab else 192
+    quant(T.pk1[:, z1:z1 + 128], T.pk1s[:, z1:z1 + 128], T.t1[:], f_t1, grp="z")
+    quant(T.pkl[:, 64:192], T.pkls[:, 64:192], T.t1[:], f_t1, grp="z")
+    fill(T.t0[:, 512:576], 0.0, grp="z")
+    zz = fill(T.tl[:, 256:512], 0.0, grp="z")
+
+    def spread(q, bank, a, col, c, *deps):
+        return cp(q, T.spr[0:16, c:512:32], T["ps%d" % bank][32 * a:32 * a + 16, col:col + 16], *deps)
+
+    def align(sp, lo, n, off, pj, extra, beside):
+        def turn(q):
+            return op("v", lambda: V.transpose(T.gr[quarter(q), :], T.spr[0:32, 128 * q:128 * q + 128]), sp)
+
+        tr = [turn(0), turn(1)]
+        last, rows = st, []
+        for i in range(16):
+            a, b = divmod(i, 4)
+            if i:
+                a0, b0 = divmod(i - 1, 4)
+                last = tt(T.um[quarter(a), b, :], T.dp[quarter(a0), b0, 0:16], T.dp[quarter(a0), b0, 1:17], ALU.max, last)
+            if i == 15:
+                dga = tt(T.dg[:, 63:15:-1], T.dp[:, 0:3, 0:16], T.dp[:, 0:3, 1:17], ALU.is_ge, rows[14])
+            last = scan(T.dp[quarter(a), b, 1:17], T.um[quarter(a), b, :], T.gr[quarter(a), 32 * b:32 * b + 16],
+                        LOW, ALU.max, ALU.add, last, tr[a])
+            rows.append(last)
+            if i < 2:
+                tr.append(turn(2 + i))
+            if i == 14:
+                dgb = tt(T.dg[0:96, 15::-1], T.dp[0:96, 3, 0:16], T.dp[0:96, 3, 1:17], ALU.is_ge, rows[11])
+            if i in beside:
+                beside[i]()
+
+        def carry(b, part, *deps):
+            k = 34 * (b + 1)
+            return tt(T.tb[part, k + 2:k + 34:2], T.dg[part, 48 - 16 * b:64 - 16 * b], T.tb[part, k + 1:k + 33:2], ALU.mult, *deps)
+
+        cy = carry(3, slice(0, 96), dgb)
+        last = tt(T.mk[:, 126::-2], T.dp[:, :, 0:16], T.um[:], ALU.is_gt, last)
+        for b in (3, 2, 1, 0):
+            if b < 3:
+                cy = carry(b, slice(0, 128), last, dga)
+            last = scan(T.tb[:, 34 * b + 2:34 * b + 34], T.mk[:, 96 - 32 * b:128 - 32 * b], T.tb[:, 34 * b + 36:34 * b + 68],
+                        T.sen[:, 0:1], ALU.mult, ALU.max, last, cy)
+
+        def seg(out, a, b, *deps):
+            return scan(out, a, b, 0.0, ALU.mult, ALU.subtract, *deps)
+
+        def cmp(a, *deps):
+            q = quarter(a)
+            return op("v", lambda: V.tensor_scalar(T.ab[q, 0:136:2], T.tb[q, 1:136:2], -16.0, T.en[q, 16:17], ALU.add, ALU.is_gt), *deps)
+
+        sg = {3: seg(T.en[64:96, :], T.rs[96:128, 0:136:2], T.tb[96:128, 1:136:2], last, extra)}
+        for a in (2, 1):
+            sg[a] = seg(T.en[quarter(a - 1), :], T.rs[quarter(a), 0:136:2], T.ab[quarter(a), 0:136:2], cmp(a, sg[a + 1]))
+        c0 = cmp(0, sg[1])
+        s0 = [seg(T.sm[0:32, k + 34:k + 136], T.rs[0:32, 34:136], T.ab[0:32, 34:136], c0) for k in (0, 544)]
+        cs = []
+        for a in (3, 2, 1):
+            for k in (0, 544):
+                cs.append(op("s", lambda a=a, k=k: S.activation(T.sm[0:32, k + 136 * a + 33:k + 136 * a + 136:34], T.en[quarter(a - 1), 16:68:17],
+                                                                AF.Identity, bias=T.pb[quarter(a - 1), :]), sg[a], st))
+        tj = op("v", lambda: V.transpose(T.jt[0:32, :], T.sm[0:32, 33:1088:34]), s0, cs)
+        p = op("s", lambda: S.activation(pj[0:32, :], T.sm[0:32, 33:544:34], AF.Identity, bias=T.nb[0:32, :]), s0[0], cs)
+        return [cp("v", off[quarter(a), :], T.jt[0:32, lo:lo + n], tj) for a in range(4)], p
+
+    def pick(dst, dsts, at, n, src, srcs, a, b, off, lst):
+        c = op("v", lambda: V.tensor_copy(dst[:, at:at + n].bitcast(dt.uint32), src[:, a:b].bitcast(dt.uint32).indirect(off)), lst)
+        s = op("s", lambda: S.activation(dsts[:, at:at + n], srcs[:, a:b].indirect(off), AF.Copy), lst)
+        return [c, s]
+
+    def unpack(x, xs, at, first, *deps):
+        return [mm(4 + b, 128, T.eq, T.eqs, 128 * b, x, xs, at, first, not first, deps[0][b] if first else [], *deps[1:]) for b in range(4)]
+
+    def halve(tile, n, col, mb, both, *deps):
+        out = []
+        for b in range(4):
+            o, i = tile[:, b:4 * n:4], T["ps%d" % (4 + b)][:, col:col + n]
+            if b % 2 == 0 and both:
+                out.append(op("v", lambda o=o, i=i: V.tensor_scalar(o, i, 0.5, None, ALU.mult), mb[b], *deps))
+            else:
+                out.append(op("s", lambda o=o, i=i: S.activation(o, i, AF.Copy, scale=0.5), mb[b], *deps))
+        return out
+
+    L, LS = T.lnd, T.lnds
+    w0 = mm(0, 128, L, LS, BO, L, LS, AO, True, True, q_o, ARRP)
+    w1 = mm(1, 128, L, LS, BO + 16, L, LS, AO, True, True)
+    w2 = mm(2, 128, L, LS, BX, L, LS, AO + 64, True, True, ARRO)
+    w3 = mm(3, 128, L, LS, BX + 16, L, LS, AO + 64, True, True)
+    unpack(L, LS, AO + 64, True, q_e)
+    sp0 = {0: [], 1: [], 2: [], 3: []}
+    for c in range(12):
+        bcol = 128 + 16 * c - 128 * (c // 4)
+        if c < 8:
+            bank, a, col = (bcol // 16) % 2, (bcol - 64) // 32, 16 * c
+        else:
+            bank, a, col = 2 + (bcol // 16) % 2, bcol // 32, 16 * c - 64
+        sp0[bank].append(spread("v" if bank % 2 == 0 else "s", bank, a, col, c, [w0, w1, w2, w3][bank], st))
+    lst0, p0 = align([sp0[k] for k in range(4)], 0, 12, T.off0, T.pj0, [], {})
+    pk0 = pick(T.pk0, T.pk0s, 0, 128, L, LS, BX, BX + 192, T.off0[:, 4:12], lst0)
+    mb0 = unpack(T.pk0, T.pk0s, 0, False, None, pk0)
+    pkl = pick(T.pkl, T.pkls, 0, 64, L, LS, BX, BX + 192, T.off0[:, 0:4], lst0)
+    h0 = halve(T.t0, 128, 0, mb0, True)
+    q0 = quant(T.q0[:], T.q0s[:], T.t0[:], h0, zz)
+    qw = []
+
+    def quant_w():
+        o = len(qw)
+        qw.append(quant(T.wq[:, 128 * o:128 * o + 128], T.wqs[:, 128 * o:128 * o + 128], T.win[:, 512 * o:512 * o + 512], ldw))
+
+    quant_w()
+    par = r >> 1
+    for u in range(8):
+        c = (4 if u % 2 == par else 0) + u // 2
+        oy = dma("y", T.pt[0:1, 16 * u:16 * u + 16], T.pj0[c:c + 1, :], p0, grp="oy")
+
+    Q, QS = T.q0, T.q0s
+    wa = mm(0, 128, Q, QS, 0, Q, QS, 0, True, True, q0, sp0[0])
+    wb = mm(1, 128, Q, QS, 16, Q, QS, 0, True, True, sp0[1])
+    unpack(L, LS, AO, True, h0)
+    mbl = unpack(T.pkl, T.pkls, 0, False, None, pkl, zz)
+    sp1 = [spread("v" if k % 2 == 0 else "s", k % 2, bb // 32 + k // 2, ab + 16 * k, 8 + k, [wa, wb][k % 2]) for k in range(4)]
+    hl = halve(T.tl, 64, 0, mbl, False)
+    unpack(Q, QS, 0, True, hl)
+    cy0 = []
+
+    def y_own():
+        quant_w()
+        for o, bank in enumerate((2, 3, 0)):
+            m = mm(bank, 128, T.wq, T.wqs, 128 * o, Q, QS, 0, True, True, qw[o], sp0[2], sp0[3], sp1 if bank == 0 else [])
+            cy0.append(cp("s", T.ys0[:, o, par:8:2, :], T["ps%d" % bank][:, 0:64], m))
+
+    def y_rest():
+        ql = quant(T.ql[:], T.qls[:], T.tl[:], hl, zz)
+        for o, bank in enumerate((2, 3, 0)):
+            m = mm(bank, 128, T.wq, T.wqs, 128 * o, T.ql, T.qls, 0, True, True, ql, cy0[o])
+            cy0.append(cp("s", T.ys0[:, o, 1 - par:8:2, :], T["ps%d" % bank][:, 0:64], m))
+            dma("y", T.y[:, 192 * o:192 * o + 128], T.ys0[:, o], cy0[o], cy0[3 + o], grp="oy")
+
+    lst1, p1 = align(sp1, 8, 4, T.off1, T.pj1, [p0], {3: quant_w, 4: y_own, 13: y_rest})
+    dma("y", T.pt[0:1, 128:192], T.pj1[8:12, :], p1, grp="oy")
+    pk1 = pick(T.pk1, T.pk1s, 128, 64, Q, QS, bb, bb + 64, T.off1[:], lst1)
+    mb1 = unpack(T.pk1, T.pk1s, 128 - ab, False, None, pk1, zz)
+    h1 = halve(T.t1, 64, ab, mb1, True, zz)
+    q1 = quant(T.q1[:], T.q1s[:], T.t1[:], h1)
+    my = [mm(1 + o, 128, T.wq, T.wqs, 128 * o, T.q1, T.q1s, 0, True, True, q1, cy0, sp1) for o in range(3)]
+    dma("y", T.oc[:], u8(T.q1[:, 0:64]), q1, grp="oy")
+    for k in range(4):
+        osd = dma("y" if k < 2 else "s", T.osc[4 * k:4 * k + 4, :], T.q1s[32 * k:32 * k + 4, 0:64], q1, grp="oy" if k < 2 else "os")
+    for o in range(3):
+        c = cp("s" if o == 1 else "v", T.ys1[:, 64 * o:64 * o + 64], T["ps%d" % (1 + o)][:, 0:64], my[o])
+        dma("s" if o == 1 else "y", T.y[:, 192 * o + 128:192 * o + 192], T.ys1[:, 64 * o:64 * o + 64], c, grp="os" if o == 1 else "oy")
+    op("y", None, oy)
+    op("s", None, osd)
+    _emit(ops, {"g": g, "v": V, "s": S, "p": P, "y": Y}, T)

@@ -21,11 +21,11 @@ SCRATCH = {
     "dn": ("sbuf", [128, 17], F32),
     "sen": ("sbuf", [128, 2], BF), "rs": ("sbuf", [128, 136], BF),
     "spr": ("sbuf", [128, 512], F32),
-    "gr": ("sbuf", [128, 128], F32),
-    "dp": ("sbuf", [128, 4, 17], F32),
+    "gr": ("sbuf", [128, 768], F32),
+    "dp": ("sbuf", [128, 5, 100], F32),
     "um": ("sbuf", [128, 4, 16], F32),
-    "dg": ("sbuf", [128, 64], BF), "mk": ("sbuf", [128, 128], BF),
-    "tb": ("sbuf", [128, 170], BF), "ab": ("sbuf", [128, 136], BF),
+    "dg": ("sbuf", [128, 4, 16], BF), "mk": ("sbuf", [128, 4, 64], BF),
+    "tb": ("sbuf", [128, 1020], BF), "ab": ("sbuf", [128, 136], BF),
     "en": ("sbuf", [128, 68], F32), "sm": ("sbuf", [128, 1088], F32),
     "jt": ("sbuf", [128, 32], F32),
     "off0": ("sbuf", [128, 12], "uint16"), "off1": ("sbuf", [128, 4], "uint16"),
@@ -42,7 +42,7 @@ SCRATCH = {
 for _k in range(8):
     SCRATCH["ps%d" % _k] = ("psum", [128, 512], F32)
 
-NSEM, POOL = 140, 8
+NSEM, POOL = 140, 12
 SEMAPHORES = ["arrp", "arro", "sent"] + ["s%d" % _k for _k in range(NSEM)]
 
 
@@ -88,7 +88,7 @@ def _emit(ops, queues, T):
         if key in waiters and key not in sem:
             if not o["grp"] and o["inc"] == 1 and waiters[key] == {o["q"]}:
                 p = pools[o["q"]]
-                if len(p) < POOL:
+                if turn[o["q"]] < POOL:
                     p.append(fresh())
                 sem[key] = p[turn[o["q"]] % POOL]
                 turn[o["q"]] += 1
@@ -119,6 +119,7 @@ def rank_program(g, core, T, topo):
         return
     V, S, P, Y = g.vector, g.scalar, g.tensor, g.sync
     ops = []
+    serial = [0]
 
     def flat(ds):
         out = []
@@ -161,6 +162,10 @@ def rank_program(g, core, T, topo):
     def quarter(a):
         return slice(32 * a, 32 * a + 32)
 
+    def group():
+        serial[0] += 1
+        return "k%d" % serial[0]
+
     BX, BO, AO, AX = 64, 128, 256, 384
     even = r % 2 == 0
     own = AO if even else BO
@@ -171,9 +176,6 @@ def rank_program(g, core, T, topo):
     f_et = fill(T.et[:], 0.0)
     f_t1 = fill(T.t1[:], 0.0)
     f_tb = fill(T.tb[:], 0.0)
-    f_ab = fill(T.ab[:], 0.0)
-    f_rs = fill(T.rs[:], 1.0)
-    fill(T.mk[:], 1.0, grp="st")
     ident = op("g", lambda: g.affine_select(T.ident[:], T.ones[:], [[-1, 128]], ALU.is_equal, 0.0, 0, 1), f_ones, grp="gs")
     op("g", lambda: g.iota(T.bas[:], [[-64, 8], [16, 4]], 128, 0, allow_small_or_imprecise_dtypes=True), grp="gs")
     op("g", lambda: g.iota(T.dn[:], [[-1, 17]], 16, 0, allow_small_or_imprecise_dtypes=True), grp="gs")
@@ -214,17 +216,21 @@ def rank_program(g, core, T, topo):
     ldw = dma("g", T.win[:], T.w[:], SENT)
 
     st = fill(T.spr[0:32, :], 0.0, grp="st")
+    f_dp = fill(T.dp[:], LOW)
+    f_ab = fill(T.ab[:], 0.0)
+    f_rs = fill(T.rs[:], 1.0)
     t_b = op("v", lambda: V.transpose(T.bt[:], T.bas[:]), ident)
     ce = [cp("v", T.et[:, 517 * k + 2:517 * k + 514:4], T.ident[:], ident, f_et) for k in range(2)]
-    fill(T.dp[:, :, 0], LOW, grp="st")
-    fill(T.um[0:32, 0, 1:16], LOW, grp="st")
-    fill(T.um[0:32, 0, 0:1], 0.0, grp="st")
+    fill(T.mk[:], 1.0, grp="st")
+    fill(T.gr[:], 0.0, grp="st")
+    fill(T.dp[0:32, 0, 1:2], 0.0, f_dp, grp="st")
     fill(T.sen[0:96, :], 17.0, grp="st")
     fill(T.sen[96:128, :], 1.0, grp="st")
     fill(T.rs[:, 0:136:34], 0.0, f_rs, grp="st")
-    fill(T.tb[0:96, 1:136:34], 17.0, f_tb, grp="st")
-    fill(T.tb[96:128, 1:136:34], 1.0, f_tb, grp="st")
-    cp("v", T.tb[0:96, 137:170:2], T.dn[0:96, :], f_tb, grp="st")
+    fill(T.tb[0:96, 6:816:204], 17.0, f_tb, grp="st")
+    fill(T.tb[96:128, 6:816:204], 1.0, f_tb, grp="st")
+    cp("v", T.tb[0:96, 822:1014:12], T.dn[0:96, 0:16], f_tb, grp="st")
+    cp("v", T.tb[0:96, 826:1018:12], T.dn[0:96, 1:17], f_tb, grp="st")
     op("v", lambda: V.tensor_scalar(T.ab[:, 1:136:34], T.bt[:, 0:4], -1.0, -16.0, ALU.mult, ALU.add), t_b, f_ab, grp="st")
     op("v", lambda: V.tensor_scalar(T.nb[:], T.bt[:, 0:1], -1.0, None, ALU.mult), t_b, grp="st")
     op("v", lambda: V.tensor_scalar(T.pb[:], T.bt[:, 0:1], 16.0, None, ALU.add), t_b, grp="st")
@@ -233,70 +239,116 @@ def rank_program(g, core, T, topo):
     for b in range(4):
         k = 516 * (b % 2) + 2 - 2 * (b // 2)
         q_e.append(quant(T.eq[:, 128 * b:128 * b + 128], T.eqs[:, 128 * b:128 * b + 128], T.et[:, k:k + 512], ce, grp="z"))
-    z1 = 0 if ab else 192
-    quant(T.pk1[:, z1:z1 + 128], T.pk1s[:, z1:z1 + 128], T.t1[:], f_t1, grp="z")
-    quant(T.pkl[:, 64:192], T.pkls[:, 64:192], T.t1[:], f_t1, grp="z")
-    fill(T.t0[:, 512:576], 0.0, grp="z")
-    zz = fill(T.tl[:, 256:512], 0.0, grp="z")
 
-    def spread(q, bank, a, col, c, *deps):
-        return cp(q, T.spr[0:16, c:512:32], T["ps%d" % bank][32 * a:32 * a + 16, col:col + 16], *deps)
+    def zeros():
+        z1 = 0 if ab else 192
+        quant(T.pk1[:, z1:z1 + 128], T.pk1s[:, z1:z1 + 128], T.t1[:], f_t1, grp="zz")
+        quant(T.pkl[:, 64:192], T.pkls[:, 64:192], T.t1[:], f_t1, grp="zz")
+
+    def zeros2():
+        fill(T.t0[:, 512:576], 0.0, grp="zz")
+        zz.append(fill(T.tl[:, 256:512], 0.0, grp="zz"))
+
+    zz = []
+
+    def spread(q, bank, a, col, c, *deps, grp=None):
+        return cp(q, T.spr[0:16, c:512:32], T["ps%d" % bank][32 * a:32 * a + 16, col:col + 16], *deps, grp=grp)
 
     def align(sp, lo, n, off, pj, extra, beside):
         def turn(q):
-            return op("v", lambda: V.transpose(T.gr[quarter(q), :], T.spr[0:32, 128 * q:128 * q + 128]), sp)
+            return op("v", lambda: V.transpose(T.gr[quarter(q), 3:768:6], T.spr[0:32, 128 * q:128 * q + 128]), sp)
 
-        tr = [turn(0), turn(1)]
-        last, rows = st, []
+        def row(i, q, slot, second, *deps):
+            a, b = divmod(i, 4)
+            step, m, at, g0 = (3, 32, (4, 0), 0) if i % 2 == 0 else (2, 48, (3, 2), 1)
+            k = at[second]
+            return scan(T.dp[quarter(q), slot, k:k + step * m - 1:step], T.dp[quarter(a), b, 1:step * m:step],
+                        T.gr[quarter(a), 192 * b + g0:192 * b + 96:step], LOW, ALU.max, ALU.add, *deps)
+
+        low, top, every = slice(0, 96), slice(96, 128), slice(0, 128)
+
+        def lfv(b, part):
+            return T.mk[part, b, 45::-3] if b % 2 else T.mk[part, b, 61::-4]
+
+        def best(b, part, *deps):
+            return tt(T.um[part, b, :], T.dp[part, b, 1:92:6], T.dp[part, b, 7:98:6], ALU.max, *deps)
+
+        def left(b, part, *deps):
+            return tt(lfv(b, part), T.dp[part, b + 1, 1:92:6], T.um[part, b, :], ALU.is_gt, *deps)
+
+        def diag(b, part, *deps):
+            return tt(T.dg[part, b, :], T.dp[part, b + 1, 1:92:6], T.dp[part, b + 1, 7:98:6], ALU.is_ge, *deps)
+
+        def either(b, part, *deps):
+            z = T.mk[part, b, 46::-3] if b % 2 else T.mk[part, b, 62::-4]
+            return tt(z, lfv(b, part), T.dg[part, b, :], ALU.max, *deps)
+
+        tr = [turn(0)]
+        last, dup, um, lf, dg, z = st, [], {}, {}, {}, {}
         for i in range(16):
             a, b = divmod(i, 4)
-            if i:
-                a0, b0 = divmod(i - 1, 4)
-                last = tt(T.um[quarter(a), b, :], T.dp[quarter(a0), b0, 0:16], T.dp[quarter(a0), b0, 1:17], ALU.max, last)
+            prev = last
             if i == 15:
-                dga = tt(T.dg[:, 63:15:-1], T.dp[:, 0:3, 0:16], T.dp[:, 0:3, 1:17], ALU.is_ge, rows[14])
-            last = scan(T.dp[quarter(a), b, 1:17], T.um[quarter(a), b, :], T.gr[quarter(a), 32 * b:32 * b + 16],
-                        LOW, ALU.max, ALU.add, last, tr[a])
-            rows.append(last)
-            if i < 2:
-                tr.append(turn(2 + i))
+                last = [row(i, a, 4, 0, prev)]
+            elif b == 3:
+                last = [row(i, a + 1, 0, k, prev) for k in (0, 1)]
+                dup.append(row(i, a, 4, 0, prev))
+            else:
+                last = [row(i, a, b + 1, k, prev, tr[a]) for k in (0, 1)]
+            if i < 3:
+                tr.append(turn(1 + i))
+            if i == 11:
+                um[3] = best(3, low, prev)
+            if i == 12:
+                lf[3], dg[3], um[0] = left(3, low, um[3], dup), diag(3, low, dup), best(0, every, prev)
+            if i == 13:
+                z[3], um[1], dg[0] = either(3, low, lf[3], dg[3]), best(1, every, prev), diag(0, every, prev)
             if i == 14:
-                dgb = tt(T.dg[0:96, 15::-1], T.dp[0:96, 3, 0:16], T.dp[0:96, 3, 1:17], ALU.is_ge, rows[11])
+                um[2], lf[0], dg[1] = best(2, every, prev), left(0, every, um[0]), diag(1, every, prev)
+            if i == 15:
+                u15, lf[2], dg[2] = best(3, top, prev), left(2, every, um[2], prev), diag(2, every, prev)
             if i in beside:
                 beside[i]()
 
-        def carry(b, part, *deps):
-            k = 34 * (b + 1)
-            return tt(T.tb[part, k + 2:k + 34:2], T.dg[part, 48 - 16 * b:64 - 16 * b], T.tb[part, k + 1:k + 33:2], ALU.mult, *deps)
+        def table(b, second, *deps):
+            k = 204 * b
+            if b % 2:
+                step, m, at, x, mask = 4, 48, (10, 1), 2, T.mk[:, b, 0:48]
+            else:
+                step, m, at, x, mask = 3, 64, (9, 1), 0, T.mk[:, b, 0:64]
+            o = k + at[second]
+            return scan(T.tb[:, o:o + step * m - 2:step], T.tb[:, k + 204 + x:k + 204 + x + step * m - 2:step], mask,
+                        T.sen[:, 0:1], ALU.max, ALU.mult, *deps)
 
-        cy = carry(3, slice(0, 96), dgb)
-        last = tt(T.mk[:, 126::-2], T.dp[:, :, 0:16], T.um[:], ALU.is_gt, last)
+        last = left(3, top, last, u15)
+        z[2], lf[1] = either(2, every, lf[2], dg[2]), left(1, every, um[1])
         for b in (3, 2, 1, 0):
-            if b < 3:
-                cy = carry(b, slice(0, 128), last, dga)
-            last = scan(T.tb[:, 34 * b + 2:34 * b + 34], T.mk[:, 96 - 32 * b:128 - 32 * b], T.tb[:, 34 * b + 36:34 * b + 68],
-                        T.sen[:, 0:1], ALU.mult, ALU.max, last, cy)
+            prev = last
+            last = [table(b, k, prev, z[b]) for k in ((0, 1) if b else (0,))]
+            if b == 3:
+                z[1], z[0] = either(1, every, lf[1], dg[1]), either(0, every, lf[0], dg[0])
 
         def seg(out, a, b, *deps):
             return scan(out, a, b, 0.0, ALU.mult, ALU.subtract, *deps)
 
         def cmp(a, *deps):
             q = quarter(a)
-            return op("v", lambda: V.tensor_scalar(T.ab[q, 0:136:2], T.tb[q, 1:136:2], -16.0, T.en[q, 16:17], ALU.add, ALU.is_gt), *deps)
+            return op("v", lambda: V.tensor_scalar(T.ab[q, 0:136:2], T.tb[q, 6:816:12], -16.0, T.en[q, 16:17], ALU.add, ALU.is_gt), *deps)
 
-        sg = {3: seg(T.en[64:96, :], T.rs[96:128, 0:136:2], T.tb[96:128, 1:136:2], last, extra)}
+        sg = {3: seg(T.en[64:96, :], T.rs[96:128, 0:136:2], T.tb[96:128, 6:816:12], last, extra)}
         for a in (2, 1):
             sg[a] = seg(T.en[quarter(a - 1), :], T.rs[quarter(a), 0:136:2], T.ab[quarter(a), 0:136:2], cmp(a, sg[a + 1]))
         c0 = cmp(0, sg[1])
         s0 = [seg(T.sm[0:32, k + 34:k + 136], T.rs[0:32, 34:136], T.ab[0:32, 34:136], c0) for k in (0, 544)]
-        cs = []
+        cs, gc = [], group()
         for a in (3, 2, 1):
             for k in (0, 544):
                 cs.append(op("s", lambda a=a, k=k: S.activation(T.sm[0:32, k + 136 * a + 33:k + 136 * a + 136:34], T.en[quarter(a - 1), 16:68:17],
-                                                                AF.Identity, bias=T.pb[quarter(a - 1), :]), sg[a], st))
+                                                                AF.Identity, bias=T.pb[quarter(a - 1), :]), sg[a], st, grp=gc))
         tj = op("v", lambda: V.transpose(T.jt[0:32, :], T.sm[0:32, 33:1088:34]), s0, cs)
         p = op("s", lambda: S.activation(pj[0:32, :], T.sm[0:32, 33:544:34], AF.Identity, bias=T.nb[0:32, :]), s0[0], cs)
-        return [cp("v", off[quarter(a), :], T.jt[0:32, lo:lo + n], tj) for a in range(4)], p
+        gl = group()
+        return [cp("v", off[quarter(a), :], T.jt[0:32, lo:lo + n], tj, grp=gl) for a in range(4)], p
 
     def pick(dst, dsts, at, n, src, srcs, a, b, off, lst):
         c = op("v", lambda: V.tensor_copy(dst[:, at:at + n].bitcast(dt.uint32), src[:, a:b].bitcast(dt.uint32).indirect(off)), lst)
@@ -329,8 +381,8 @@ def rank_program(g, core, T, topo):
             bank, a, col = (bcol // 16) % 2, (bcol - 64) // 32, 16 * c
         else:
             bank, a, col = 2 + (bcol // 16) % 2, bcol // 32, 16 * c - 64
-        sp0[bank].append(spread("v" if bank % 2 == 0 else "s", bank, a, col, c, [w0, w1, w2, w3][bank], st))
-    lst0, p0 = align([sp0[k] for k in range(4)], 0, 12, T.off0, T.pj0, [], {})
+        sp0[bank].append(spread("v" if bank % 2 == 0 else "s", bank, a, col, c, [w0, w1, w2, w3][bank], st, grp="sp%d" % (bank % 2)))
+    lst0, p0 = align([sp0[k] for k in range(4)], 0, 12, T.off0, T.pj0, [], {4: zeros, 5: zeros2})
     pk0 = pick(T.pk0, T.pk0s, 0, 128, L, LS, BX, BX + 192, T.off0[:, 4:12], lst0)
     mb0 = unpack(T.pk0, T.pk0s, 0, False, None, pk0)
     pkl = pick(T.pkl, T.pkls, 0, 64, L, LS, BX, BX + 192, T.off0[:, 0:4], lst0)
@@ -353,7 +405,7 @@ def rank_program(g, core, T, topo):
     wb = mm(1, 128, Q, QS, 16, Q, QS, 0, True, True, sp0[1])
     unpack(L, LS, AO, True, h0)
     mbl = unpack(T.pkl, T.pkls, 0, False, None, pkl, zz)
-    sp1 = [spread("v" if k % 2 == 0 else "s", k % 2, bb // 32 + k // 2, ab + 16 * k, 8 + k, [wa, wb][k % 2]) for k in range(4)]
+    sp1 = [spread("v" if k % 2 == 0 else "s", k % 2, bb // 32 + k // 2, ab + 16 * k, 8 + k, [wa, wb][k % 2], grp="sq%d" % (k % 2)) for k in range(4)]
     hl = halve(T.tl, 64, 0, mbl, False)
     unpack(Q, QS, 0, True, hl)
     cy0 = []
@@ -371,7 +423,7 @@ def rank_program(g, core, T, topo):
             cy0.append(cp("s", T.ys0[:, o, 1 - par:8:2, :], T["ps%d" % bank][:, 0:64], m))
             dma("y", T.y[:, 192 * o:192 * o + 128], T.ys0[:, o], cy0[o], cy0[3 + o], grp="oy")
 
-    lst1, p1 = align(sp1, 8, 4, T.off1, T.pj1, [p0], {3: quant_w, 4: y_own, 13: y_rest})
+    lst1, p1 = align(sp1, 8, 4, T.off1, T.pj1, [p0], {4: quant_w, 5: y_own, 10: y_rest})
     dma("y", T.pt[0:1, 128:192], T.pj1[8:12, :], p1, grp="oy")
     pk1 = pick(T.pk1, T.pk1s, 128, 64, Q, QS, bb, bb + 64, T.off1[:], lst1)
     mb1 = unpack(T.pk1, T.pk1s, 128 - ab, False, None, pk1, zz)

@@ -27,12 +27,11 @@ SCRATCH = {
     "dg": ("sbuf", [128, 4, 16], BF), "mk": ("sbuf", [128, 4, 64], BF),
     "tb": ("sbuf", [128, 1020], BF), "ab": ("sbuf", [128, 136], BF),
     "en": ("sbuf", [128, 68], F32), "sm": ("sbuf", [128, 1088], F32),
-    "jt": ("sbuf", [128, 32], F32),
+    "e2": ("sbuf", [128, 17], F32), "ev": ("sbuf", [128, 1], F32), "sgn": ("sbuf", [128, 49], F32),
+    "jt": ("sbuf", [128, 32], F32), "ju": ("sbuf", [128, 32], F32), "jv": ("sbuf", [128, 32], F32),
     "off0": ("sbuf", [128, 12], "uint16"), "off1": ("sbuf", [128, 4], "uint16"),
-    "pj0": ("sbuf", [128, 16], F32), "pj1": ("sbuf", [128, 16], F32),
-    "pk0": ("sbuf", [128, 128], X4), "pk0s": ("sbuf", [128, 128], U8),
-    "pkl": ("sbuf", [128, 192], X4), "pkls": ("sbuf", [128, 192], U8),
-    "pk1": ("sbuf", [128, 320], X4), "pk1s": ("sbuf", [128, 320], U8),
+    "pj1": ("sbuf", [128, 16], F32),
+    "hf0": ("sbuf", [128, 1536], F32), "hf1": ("sbuf", [128, 512], F32),
     "t0": ("sbuf", [128, 576], BF), "tl": ("sbuf", [128, 512], BF), "t1": ("sbuf", [128, 512], BF),
     "q0": ("sbuf", [128, 144], X4), "q0s": ("sbuf", [128, 144], U8),
     "ql": ("sbuf", [128, 128], X4), "qls": ("sbuf", [128, 128], U8),
@@ -86,7 +85,7 @@ def _emit(ops, queues, T):
     for i, o in enumerate(ops):
         key = o["grp"] or i
         if key in waiters and key not in sem:
-            if not o["grp"] and o["inc"] == 1 and waiters[key] == {o["q"]}:
+            if (not o["grp"] or o["grp"][0] == "p") and o["inc"] == 1 and waiters[key] == {o["q"]}:
                 p = pools[o["q"]]
                 if turn[o["q"]] < POOL:
                     p.append(fresh())
@@ -149,22 +148,22 @@ def rank_program(g, core, T, topo):
     def quant(out, sc, in_, *deps, grp=None):
         return op("v", lambda: V.quantize_mx(out, sc, in_), *deps, grp=grp)
 
-    def mm(bank, n, w, ws, a, x, xs, b, start, stop, *deps):
+    def mm(bank, n, w, ws, a, x, xs, b, *deps):
         return op("p", lambda: P.matmul_mx(T["ps%d" % bank][:, 0:n], w[:, a:a + 128], ws[:, a:a + 128],
-                                           x[:, b:b + n], xs[:, b:b + n], start, stop), *deps)
+                                           x[:, b:b + n], xs[:, b:b + n], True, True), *deps)
 
-    def tt(out, a, b, o, *deps):
-        return op("v", lambda: V.tensor_tensor(out, a, b, o), *deps)
+    def tt(out, a, b, o, *deps, grp=None):
+        return op("v", lambda: V.tensor_tensor(out, a, b, o), *deps, grp=grp)
 
-    def scan(out, a, b, init, o0, o1, *deps):
-        return op("v", lambda: V.tensor_tensor_scan(out, a, b, init, o0, o1), *deps)
+    def scan(out, a, b, init, o0, o1, *deps, grp=None):
+        return op("v", lambda: V.tensor_tensor_scan(out, a, b, init, o0, o1), *deps, grp=grp)
 
     def quarter(a):
         return slice(32 * a, 32 * a + 32)
 
     def group():
         serial[0] += 1
-        return "k%d" % serial[0]
+        return "p%d" % serial[0]
 
     BX, BO, AO, AX = 64, 128, 256, 384
     even = r % 2 == 0
@@ -174,16 +173,16 @@ def rank_program(g, core, T, topo):
     ldx = dma("y", T.xin[:], T.x[:])
     f_ones = fill(T.ones[:], 1.0)
     f_et = fill(T.et[:], 0.0)
-    f_t1 = fill(T.t1[:], 0.0)
     f_tb = fill(T.tb[:], 0.0)
+    f_dp = fill(T.dp[:], LOW)
     ident = op("g", lambda: g.affine_select(T.ident[:], T.ones[:], [[-1, 128]], ALU.is_equal, 0.0, 0, 1), f_ones, grp="gs")
     op("g", lambda: g.iota(T.bas[:], [[-64, 8], [16, 4]], 128, 0, allow_small_or_imprecise_dtypes=True), grp="gs")
-    op("g", lambda: g.iota(T.dn[:], [[-1, 17]], 16, 0, allow_small_or_imprecise_dtypes=True), grp="gs")
+    op("g", lambda: g.iota(T.dn[:], [[-1, 17]], 24, 0, allow_small_or_imprecise_dtypes=True), grp="gs")
 
     order = [r ^ 3, r ^ 1, r ^ 2, r] if even else [r ^ 1, r ^ 3, r, r ^ 2]
-    cx = [cp("v" if k < 2 else "s", T.xt[:, 256 * k:256 * k + 256], T.xin[:, :, order[k], :], ldx) for k in range(4)]
-    q_s = quant(T.snd[:], T.snds[:], T.xt[:, 0:512], cx[0], cx[1])
-    q_o = quant(T.lnd[:, own:own + 128], T.lnds[:, own:own + 128], T.xt[:, 512:1024], cx[2], cx[3])
+    cx = [cp("v" if k < 2 else "s", T.xt[:, 256 * k:256 * k + 256], T.xin[:, :, order[k], :], ldx, grp="px%d" % (k // 2)) for k in range(4)]
+    q_s = quant(T.snd[:], T.snds[:], T.xt[:, 0:512], cx[0])
+    q_o = quant(T.lnd[:, own:own + 128], T.lnds[:, own:own + 128], T.xt[:, 512:1024], cx[2])
 
     def u8(v):
         return v.bitcast(dt.uint8)
@@ -216,7 +215,6 @@ def rank_program(g, core, T, topo):
     ldw = dma("g", T.win[:], T.w[:], SENT)
 
     st = fill(T.spr[0:32, :], 0.0, grp="st")
-    f_dp = fill(T.dp[:], LOW)
     f_ab = fill(T.ab[:], 0.0)
     f_rs = fill(T.rs[:], 1.0)
     t_b = op("v", lambda: V.transpose(T.bt[:], T.bas[:]), ident)
@@ -224,10 +222,10 @@ def rank_program(g, core, T, topo):
     fill(T.mk[:], 1.0, grp="st")
     fill(T.gr[:], 0.0, grp="st")
     fill(T.dp[0:32, 0, 1:2], 0.0, f_dp, grp="st")
-    fill(T.sen[0:96, :], 17.0, grp="st")
+    fill(T.sen[0:96, :], 25.0, grp="st")
     fill(T.sen[96:128, :], 1.0, grp="st")
     fill(T.rs[:, 0:136:34], 0.0, f_rs, grp="st")
-    fill(T.tb[0:96, 6:816:204], 17.0, f_tb, grp="st")
+    fill(T.tb[0:96, 6:816:204], 25.0, f_tb, grp="st")
     fill(T.tb[96:128, 6:816:204], 1.0, f_tb, grp="st")
     cp("v", T.tb[0:96, 822:1014:12], T.dn[0:96, 0:16], f_tb, grp="st")
     cp("v", T.tb[0:96, 826:1018:12], T.dn[0:96, 1:17], f_tb, grp="st")
@@ -235,18 +233,16 @@ def rank_program(g, core, T, topo):
     op("v", lambda: V.tensor_scalar(T.nb[:], T.bt[:, 0:1], -1.0, None, ALU.mult), t_b, grp="st")
     op("v", lambda: V.tensor_scalar(T.pb[:], T.bt[:, 0:1], 16.0, None, ALU.add), t_b, grp="st")
     cp("v", T.sm[0:32, 33:1088:544], T.bt[0:32, 0:2], t_b, grp="st")
-    q_e = []
     for b in range(4):
         k = 516 * (b % 2) + 2 - 2 * (b // 2)
-        q_e.append(quant(T.eq[:, 128 * b:128 * b + 128], T.eqs[:, 128 * b:128 * b + 128], T.et[:, k:k + 512], ce, grp="z"))
+        q_e = quant(T.eq[:, 128 * b:128 * b + 128], T.eqs[:, 128 * b:128 * b + 128], T.et[:, k:k + 512], ce, grp="z")
 
     def zeros():
-        z1 = 0 if ab else 192
-        quant(T.pk1[:, z1:z1 + 128], T.pk1s[:, z1:z1 + 128], T.t1[:], f_t1, grp="zz")
-        quant(T.pkl[:, 64:192], T.pkls[:, 64:192], T.t1[:], f_t1, grp="zz")
+        fill(T.t0[:, 512:576], 0.0, grp="zz")
+        fill(T.ju[0:32, 8:32], 0.0, grp="zz")
 
     def zeros2():
-        fill(T.t0[:, 512:576], 0.0, grp="zz")
+        fill(T.t1[:, 256:512], 0.0, grp="zz")
         zz.append(fill(T.tl[:, 256:512], 0.0, grp="zz"))
 
     zz = []
@@ -254,16 +250,16 @@ def rank_program(g, core, T, topo):
     def spread(q, bank, a, col, c, *deps, grp=None):
         return cp(q, T.spr[0:16, c:512:32], T["ps%d" % bank][32 * a:32 * a + 16, col:col + 16], *deps, grp=grp)
 
-    def align(sp, lo, n, off, pj, extra, beside):
+    def align(sp, lo, n, off, beside):
         def turn(q):
             return op("v", lambda: V.transpose(T.gr[quarter(q), 3:768:6], T.spr[0:32, 128 * q:128 * q + 128]), sp)
 
-        def row(i, q, slot, second, *deps):
+        def row(i, q, slot, second, *deps, grp=None):
             a, b = divmod(i, 4)
             step, m, at, g0 = (3, 32, (4, 0), 0) if i % 2 == 0 else (2, 48, (3, 2), 1)
             k = at[second]
             return scan(T.dp[quarter(q), slot, k:k + step * m - 1:step], T.dp[quarter(a), b, 1:step * m:step],
-                        T.gr[quarter(a), 192 * b + g0:192 * b + 96:step], LOW, ALU.max, ALU.add, *deps)
+                        T.gr[quarter(a), 192 * b + g0:192 * b + 96:step], LOW, ALU.max, ALU.add, *deps, grp=grp)
 
         low, top, every = slice(0, 96), slice(96, 128), slice(0, 128)
 
@@ -287,14 +283,14 @@ def rank_program(g, core, T, topo):
         last, dup, um, lf, dg, z = st, [], {}, {}, {}, {}
         for i in range(16):
             a, b = divmod(i, 4)
-            prev = last
+            prev, gr = last, group()
             if i == 15:
                 last = [row(i, a, 4, 0, prev)]
             elif b == 3:
-                last = [row(i, a + 1, 0, k, prev) for k in (0, 1)]
+                last = [row(i, a + 1, 0, k, prev, grp=gr) for k in (0, 1)]
                 dup.append(row(i, a, 4, 0, prev))
             else:
-                last = [row(i, a, b + 1, k, prev, tr[a]) for k in (0, 1)]
+                last = [row(i, a, b + 1, k, prev, tr[a], grp=gr) for k in (0, 1)]
             if i < 3:
                 tr.append(turn(1 + i))
             if i == 11:
@@ -310,7 +306,7 @@ def rank_program(g, core, T, topo):
             if i in beside:
                 beside[i]()
 
-        def table(b, second, *deps):
+        def table(b, second, *deps, grp=None):
             k = 204 * b
             if b % 2:
                 step, m, at, x, mask = 4, 48, (10, 1), 2, T.mk[:, b, 0:48]
@@ -318,62 +314,67 @@ def rank_program(g, core, T, topo):
                 step, m, at, x, mask = 3, 64, (9, 1), 0, T.mk[:, b, 0:64]
             o = k + at[second]
             return scan(T.tb[:, o:o + step * m - 2:step], T.tb[:, k + 204 + x:k + 204 + x + step * m - 2:step], mask,
-                        T.sen[:, 0:1], ALU.max, ALU.mult, *deps)
+                        T.sen[:, 0:1], ALU.max, ALU.mult, *deps, grp=grp)
 
         last = left(3, top, last, u15)
         z[2], lf[1] = either(2, every, lf[2], dg[2]), left(1, every, um[1])
         for b in (3, 2, 1, 0):
-            prev = last
-            last = [table(b, k, prev, z[b]) for k in ((0, 1) if b else (0,))]
+            prev, gr = last, group()
+            last = [table(b, k, prev, z[b], grp=gr) for k in ((0, 1) if b else (0,))]
             if b == 3:
                 z[1], z[0] = either(1, every, lf[1], dg[1]), either(0, every, lf[0], dg[0])
 
-        def seg(out, a, b, *deps):
-            return scan(out, a, b, 0.0, ALU.mult, ALU.subtract, *deps)
+        gs = group()
 
-        def cmp(a, *deps):
+        def seg(a, *deps):
+            f = 0 if a else 34
+            return [scan(T.sm[0:32, k + 136 * a + f:k + 136 * a + 136], T.rs[quarter(a), f:136], T.ab[quarter(a), f:136],
+                         0.0, ALU.mult, ALU.subtract, *deps, grp=gs) for k in (0, 544)]
+
+        def cmp(a, c, e, *deps):
             q = quarter(a)
-            return op("v", lambda: V.tensor_scalar(T.ab[q, 0:136:2], T.tb[q, 6:816:12], -16.0, T.en[q, 16:17], ALU.add, ALU.is_gt), *deps)
+            return op("v", lambda: V.tensor_scalar(T.ab[q, 0:136:2], T.tb[q, 6:816:12], c, e, ALU.mult, ALU.is_gt), *deps)
 
-        sg = {3: seg(T.en[64:96, :], T.rs[96:128, 0:136:2], T.tb[96:128, 6:816:12], last, extra)}
-        for a in (2, 1):
-            sg[a] = seg(T.en[quarter(a - 1), :], T.rs[quarter(a), 0:136:2], T.ab[quarter(a), 0:136:2], cmp(a, sg[a + 1]))
-        c0 = cmp(0, sg[1])
-        s0 = [seg(T.sm[0:32, k + 34:k + 136], T.rs[0:32, 34:136], T.ab[0:32, 34:136], c0) for k in (0, 544)]
+        def look(a, c, e, *deps):
+            return op("s", lambda: S.activation(T.sgn[quarter(a - 1), :], T.tb[quarter(a), 6:199:4], AF.Sign, bias=e, scale=c,
+                                                accum_out=T.ev[quarter(a - 1), :]), *deps)
+
+        e2, e1, e0 = T.e2[64:96, 16:17], T.ev[32:64, :], T.ev[0:32, :]
+        j12 = scan(T.e2[64:96, :], T.ones[96:128, 0:17], T.tb[96:128, 6:210:12], 24.5, ALU.mult, ALU.subtract, last)
+        s3 = scan(T.en[64:96, :], T.rs[96:128, 0:136:2], T.tb[96:128, 6:816:12], 0.0, ALU.mult, ALU.subtract, last)
+        j8 = look(2, -1.0, e2, j12)
         cs, gc = [], group()
-        for a in (3, 2, 1):
-            for k in (0, 544):
-                cs.append(op("s", lambda a=a, k=k: S.activation(T.sm[0:32, k + 136 * a + 33:k + 136 * a + 136:34], T.en[quarter(a - 1), 16:68:17],
-                                                                AF.Identity, bias=T.pb[quarter(a - 1), :]), sg[a], st, grp=gc))
+        for k in (0, 544):
+            cs.append(op("s", lambda k=k: S.activation(T.sm[0:32, k + 441:k + 544:34], T.en[64:96, 16:68:17],
+                                                       AF.Identity, bias=T.pb[64:96, :]), s3, st, grp=gc))
+        j4 = look(1, -2.0, e1, j8)
+        c2 = cmp(2, 1.0, e2, j12)
+        c1 = cmp(1, 2.0, e1, j8)
+        seg(2, c2)
+        c0 = cmp(0, 2.0, e0, j4)
+        seg(1, c1)
+        s0 = seg(0, c0)
         tj = op("v", lambda: V.transpose(T.jt[0:32, :], T.sm[0:32, 33:1088:34]), s0, cs)
-        p = op("s", lambda: S.activation(pj[0:32, :], T.sm[0:32, 33:544:34], AF.Identity, bias=T.nb[0:32, :]), s0[0], cs)
         gl = group()
-        return [cp("v", off[quarter(a), :], T.jt[0:32, lo:lo + n], tj, grp=gl) for a in range(4)], p
+        return [cp("v", off[quarter(a), :], T.jt[0:32, lo:lo + n], tj, grp=gl) for a in range(4)], [s0, cs], tj
 
-    def pick(dst, dsts, at, n, src, srcs, a, b, off, lst):
-        c = op("v", lambda: V.tensor_copy(dst[:, at:at + n].bitcast(dt.uint32), src[:, a:b].bitcast(dt.uint32).indirect(off)), lst)
-        s = op("s", lambda: S.activation(dsts[:, at:at + n], srcs[:, a:b].indirect(off), AF.Copy), lst)
-        return [c, s]
-
-    def unpack(x, xs, at, first, *deps):
-        return [mm(4 + b, 128, T.eq, T.eqs, 128 * b, x, xs, at, first, not first, deps[0][b] if first else [], *deps[1:]) for b in range(4)]
-
-    def halve(tile, n, col, mb, both, *deps):
+    def unpack(hf, n, x, xs, at, *deps):
+        gu = group()
         out = []
         for b in range(4):
-            o, i = tile[:, b:4 * n:4], T["ps%d" % (4 + b)][:, col:col + n]
-            if b % 2 == 0 and both:
-                out.append(op("v", lambda o=o, i=i: V.tensor_scalar(o, i, 0.5, None, ALU.mult), mb[b], *deps))
-            else:
-                out.append(op("s", lambda o=o, i=i: S.activation(o, i, AF.Copy, scale=0.5), mb[b], *deps))
+            m = mm(4 + b, n, T.eq, T.eqs, 128 * b, x, xs, at, *deps)
+            out.append(op("s", lambda b=b: S.activation(hf[:, n * b:n * b + n], T["ps%d" % (4 + b)][:, 0:n], AF.Copy, scale=0.5), m, grp=gu))
         return out
 
+    def blend(tile, n, hf, w, a, b0, b1, off, bs, *deps, grp=None):
+        return [tt(tile[:, b:4 * n:4], hf[:, w * b + b0:w * b + b1].indirect(off), hf[:, w * b + a:w * b + a + n], ALU.add, *deps, grp=grp)
+                for b in bs]
+
     L, LS = T.lnd, T.lnds
-    w0 = mm(0, 128, L, LS, BO, L, LS, AO, True, True, q_o, ARRP)
-    w1 = mm(1, 128, L, LS, BO + 16, L, LS, AO, True, True)
-    w2 = mm(2, 128, L, LS, BX, L, LS, AO + 64, True, True, ARRO)
-    w3 = mm(3, 128, L, LS, BX + 16, L, LS, AO + 64, True, True)
-    unpack(L, LS, AO + 64, True, q_e)
+    w0 = mm(0, 128, L, LS, BO, L, LS, AO, q_o, ARRP)
+    w1 = mm(1, 128, L, LS, BO + 16, L, LS, AO)
+    w2 = mm(2, 128, L, LS, BX, L, LS, AO + 64, ARRO)
+    w3 = mm(3, 128, L, LS, BX + 16, L, LS, AO + 64)
     sp0 = {0: [], 1: [], 2: [], 3: []}
     for c in range(12):
         bcol = 128 + 16 * c - 128 * (c // 4)
@@ -382,12 +383,15 @@ def rank_program(g, core, T, topo):
         else:
             bank, a, col = 2 + (bcol // 16) % 2, bcol // 32, 16 * c - 64
         sp0[bank].append(spread("v" if bank % 2 == 0 else "s", bank, a, col, c, [w0, w1, w2, w3][bank], st, grp="sp%d" % (bank % 2)))
-    lst0, p0 = align([sp0[k] for k in range(4)], 0, 12, T.off0, T.pj0, [], {4: zeros, 5: zeros2})
-    pk0 = pick(T.pk0, T.pk0s, 0, 128, L, LS, BX, BX + 192, T.off0[:, 4:12], lst0)
-    mb0 = unpack(T.pk0, T.pk0s, 0, False, None, pk0)
-    pkl = pick(T.pkl, T.pkls, 0, 64, L, LS, BX, BX + 192, T.off0[:, 0:4], lst0)
-    h0 = halve(T.t0, 128, 0, mb0, True)
+    u0 = unpack(T.hf0, 384, L, LS, BX, q_e)
+    lst0, _, tj0 = align([sp0[k] for k in range(4)], 0, 12, T.off0, {4: zeros, 5: zeros2})
+    h0 = blend(T.t0, 128, T.hf0, 384, 256, 0, 192, T.off0[:, 4:12], range(4), lst0, u0, grp=group())
+    par = r >> 1
+    ju = [tt(T.ju[0:32, par:8:2], T.jt[0:32, 4:8], T.bas[0:32, 4:8], ALU.subtract, tj0),
+          tt(T.ju[0:32, 1 - par:8:2], T.jt[0:32, 0:4], T.bas[0:32, 0:4], ALU.subtract, tj0)]
     q0 = quant(T.q0[:], T.q0s[:], T.t0[:], h0, zz)
+    jv = op("v", lambda: V.transpose(T.jv[0:32, :], T.ju[0:32, :]), ju, zz)
+    oy = dma("y", T.pt[0:1, 0:128], T.jv[0:8, 0:16], jv, grp="oy")
     qw = []
 
     def quant_w():
@@ -395,47 +399,44 @@ def rank_program(g, core, T, topo):
         qw.append(quant(T.wq[:, 128 * o:128 * o + 128], T.wqs[:, 128 * o:128 * o + 128], T.win[:, 512 * o:512 * o + 512], ldw))
 
     quant_w()
-    par = r >> 1
-    for u in range(8):
-        c = (4 if u % 2 == par else 0) + u // 2
-        oy = dma("y", T.pt[0:1, 16 * u:16 * u + 16], T.pj0[c:c + 1, :], p0, grp="oy")
+    quant_w()
 
     Q, QS = T.q0, T.q0s
-    wa = mm(0, 128, Q, QS, 0, Q, QS, 0, True, True, q0, sp0[0])
-    wb = mm(1, 128, Q, QS, 16, Q, QS, 0, True, True, sp0[1])
-    unpack(L, LS, AO, True, h0)
-    mbl = unpack(T.pkl, T.pkls, 0, False, None, pkl, zz)
+    wa = mm(0, 128, Q, QS, 0, Q, QS, 0, q0, sp0[0])
+    wb = mm(1, 128, Q, QS, 16, Q, QS, 0, sp0[1])
     sp1 = [spread("v" if k % 2 == 0 else "s", k % 2, bb // 32 + k // 2, ab + 16 * k, 8 + k, [wa, wb][k % 2], grp="sq%d" % (k % 2)) for k in range(4)]
-    hl = halve(T.tl, 64, 0, mbl, False)
-    unpack(Q, QS, 0, True, hl)
-    cy0 = []
+    u1 = unpack(T.hf1, 128, Q, QS, 0, u0)
+    cy0, hl = [], []
 
     def y_own():
         quant_w()
         for o, bank in enumerate((2, 3, 0)):
-            m = mm(bank, 128, T.wq, T.wqs, 128 * o, Q, QS, 0, True, True, qw[o], sp0[2], sp0[3], sp1 if bank == 0 else [])
+            m = mm(bank, 128, T.wq, T.wqs, 128 * o, Q, QS, 0, qw[o], sp0[2], sp0[3], sp1 if bank == 0 else [])
             cy0.append(cp("s", T.ys0[:, o, par:8:2, :], T["ps%d" % bank][:, 0:64], m))
+
+    def rest():
+        hl.append(blend(T.tl, 64, T.hf0, 384, 192, 0, 192, T.off0[:, 0:4], [len(hl)], lst0, u0))
 
     def y_rest():
         ql = quant(T.ql[:], T.qls[:], T.tl[:], hl, zz)
         for o, bank in enumerate((2, 3, 0)):
-            m = mm(bank, 128, T.wq, T.wqs, 128 * o, T.ql, T.qls, 0, True, True, ql, cy0[o])
+            m = mm(bank, 128, T.wq, T.wqs, 128 * o, T.ql, T.qls, 0, ql, cy0[o])
             cy0.append(cp("s", T.ys0[:, o, 1 - par:8:2, :], T["ps%d" % bank][:, 0:64], m))
             dma("y", T.y[:, 192 * o:192 * o + 128], T.ys0[:, o], cy0[o], cy0[3 + o], grp="oy")
 
-    lst1, p1 = align(sp1, 8, 4, T.off1, T.pj1, [p0], {4: quant_w, 5: y_own, 10: y_rest})
-    dma("y", T.pt[0:1, 128:192], T.pj1[8:12, :], p1, grp="oy")
-    pk1 = pick(T.pk1, T.pk1s, 128, 64, Q, QS, bb, bb + 64, T.off1[:], lst1)
-    mb1 = unpack(T.pk1, T.pk1s, 128 - ab, False, None, pk1, zz)
-    h1 = halve(T.t1, 64, ab, mb1, True, zz)
-    q1 = quant(T.q1[:], T.q1s[:], T.t1[:], h1)
-    my = [mm(1 + o, 128, T.wq, T.wqs, 128 * o, T.q1, T.q1s, 0, True, True, q1, cy0, sp1) for o in range(3)]
+    lst1, sm1, _ = align(sp1, 8, 4, T.off1, {4: y_own, 5: rest, 6: rest, 8: rest, 9: rest, 10: y_rest})
+    p1 = op("s", lambda: S.activation(T.pj1[0:32, :], T.sm[0:32, 33:544:34], AF.Identity, bias=T.nb[0:32, :]), sm1)
+    og = dma("g", T.pt[0:1, 128:192], T.pj1[8:12, :], p1, grp="og")
+    h1 = blend(T.t1, 64, T.hf1, 128, ab, bb, bb + 64, T.off1[:], range(4), lst1, u1, grp=group())
+    q1 = quant(T.q1[:], T.q1s[:], T.t1[:], h1, zz)
+    my = [mm(1 + o, 128, T.wq, T.wqs, 128 * o, T.q1, T.q1s, 0, q1, cy0, sp1) for o in range(3)]
     dma("y", T.oc[:], u8(T.q1[:, 0:64]), q1, grp="oy")
     for k in range(4):
-        osd = dma("y" if k < 2 else "s", T.osc[4 * k:4 * k + 4, :], T.q1s[32 * k:32 * k + 4, 0:64], q1, grp="oy" if k < 2 else "os")
+        osd = dma("y" if k < 1 else "s", T.osc[4 * k:4 * k + 4, :], T.q1s[32 * k:32 * k + 4, 0:64], q1, grp="oy" if k < 1 else "os")
     for o in range(3):
-        c = cp("s" if o == 1 else "v", T.ys1[:, 64 * o:64 * o + 64], T["ps%d" % (1 + o)][:, 0:64], my[o])
+        c = cp("v", T.ys1[:, 64 * o:64 * o + 64], T["ps%d" % (1 + o)][:, 0:64], my[o])
         dma("s" if o == 1 else "y", T.y[:, 192 * o + 128:192 * o + 192], T.ys1[:, 64 * o:64 * o + 64], c, grp="os" if o == 1 else "oy")
     op("y", None, oy)
     op("s", None, osd)
+    op("g", None, og)
     _emit(ops, {"g": g, "v": V, "s": S, "p": P, "y": Y}, T)

@@ -13,25 +13,26 @@ SCRATCH = {
     "lnd": ("sbuf", [128, 512], X4), "lnds": ("sbuf", [128, 512], U8),
     "win": ("sbuf", [128, 1536], BF),
     "wq": ("sbuf", [128, 384], X4), "wqs": ("sbuf", [128, 384], U8),
-    "ones": ("sbuf", [128, 128], BF), "ident": ("sbuf", [128, 128], BF),
+    "ones": ("sbuf", [128, 128], BF), "half": ("sbuf", [128, 128], BF), "ident": ("sbuf", [128, 128], BF),
     "et": ("sbuf", [128, 1032], BF),
     "eq": ("sbuf", [128, 512], X4), "eqs": ("sbuf", [128, 512], U8),
     "bas": ("sbuf", [128, 32], F32), "bt": ("sbuf", [128, 32], F32),
-    "nb": ("sbuf", [128, 1], F32), "pb": ("sbuf", [128, 1], F32),
-    "dn": ("sbuf", [128, 17], F32),
-    "sen": ("sbuf", [128, 2], BF), "rs": ("sbuf", [128, 136], BF),
+    "nb": ("sbuf", [128, 1], F32),
+    "sen": ("sbuf", [128, 2], BF), "rs": ("sbuf", [128, 68], BF),
     "spr": ("sbuf", [128, 512], F32),
-    "gr": ("sbuf", [128, 768], F32),
-    "dp": ("sbuf", [128, 5, 100], F32),
+    "gr": ("sbuf", [128, 1920], F32),
+    "dp": ("sbuf", [128, 6, 216], F32),
     "um": ("sbuf", [128, 4, 16], F32),
-    "dg": ("sbuf", [128, 4, 16], BF), "mk": ("sbuf", [128, 4, 64], BF),
-    "tb": ("sbuf", [128, 1020], BF), "ab": ("sbuf", [128, 136], BF),
-    "en": ("sbuf", [128, 68], F32), "sm": ("sbuf", [128, 1088], F32),
-    "e2": ("sbuf", [128, 17], F32), "ev": ("sbuf", [128, 1], F32), "sgn": ("sbuf", [128, 49], F32),
+    "dg": ("sbuf", [128, 4, 16], BF), "mk": ("sbuf", [128, 4, 160], BF),
+    "tb": ("sbuf", [128, 1536], BF),
+    "ab": ("sbuf", [128, 68], BF),
+    "sm": ("sbuf", [128, 544], F32),
+    "e2": ("sbuf", [128, 16], F32), "ev": ("sbuf", [128, 1], F32), "sgn": ("sbuf", [128, 33], F32),
     "jt": ("sbuf", [128, 32], F32), "ju": ("sbuf", [128, 32], F32), "jv": ("sbuf", [128, 32], F32),
     "off0": ("sbuf", [128, 12], "uint16"), "off1": ("sbuf", [128, 4], "uint16"),
     "pj1": ("sbuf", [128, 16], F32),
     "hf0": ("sbuf", [128, 1536], F32), "hf1": ("sbuf", [128, 512], F32),
+    "pk0": ("sbuf", [128, 256], F32), "pk1": ("sbuf", [128, 64], F32),
     "t0": ("sbuf", [128, 576], BF), "tl": ("sbuf", [128, 512], BF), "t1": ("sbuf", [128, 512], BF),
     "q0": ("sbuf", [128, 144], X4), "q0s": ("sbuf", [128, 144], U8),
     "ql": ("sbuf", [128, 128], X4), "qls": ("sbuf", [128, 128], U8),
@@ -41,7 +42,7 @@ SCRATCH = {
 for _k in range(8):
     SCRATCH["ps%d" % _k] = ("psum", [128, 512], F32)
 
-NSEM, POOL = 140, 12
+NSEM = 140
 SEMAPHORES = ["arrp", "arro", "sent"] + ["s%d" % _k for _k in range(NSEM)]
 
 
@@ -79,18 +80,23 @@ def _emit(ops, queues, T):
         nxt[0] += 1
         return "s%d" % (nxt[0] - 1)
 
+    final = {}
+    for i, o in enumerate(ops):
+        for d in o["waits"]:
+            if not isinstance(d, tuple):
+                final[ops[d]["grp"] or d] = i
     pools = {q: [] for q in queues}
-    turn = {q: 0 for q in queues}
     sem, total = {}, {}
     for i, o in enumerate(ops):
         key = o["grp"] or i
         if key in waiters and key not in sem:
             if (not o["grp"] or o["grp"][0] == "p") and o["inc"] == 1 and waiters[key] == {o["q"]}:
-                p = pools[o["q"]]
-                if turn[o["q"]] < POOL:
-                    p.append(fresh())
-                sem[key] = p[turn[o["q"]] % POOL]
-                turn[o["q"]] += 1
+                p = [e for e in pools[o["q"]] if e[1] <= i]
+                if not p:
+                    p = [[fresh(), 0]]
+                    pools[o["q"]].append(p[0])
+                sem[key] = p[0][0]
+                p[0][1] = final[key]
             else:
                 sem[key] = fresh()
                 total[key] = sum(ops[m]["inc"] for m in members[key]) if o["grp"] else o["inc"]
@@ -171,13 +177,12 @@ def rank_program(g, core, T, topo):
     ab, bb = (0, 64) if r < 2 else (64, 0)
 
     ldx = dma("y", T.xin[:], T.x[:])
-    f_ones = fill(T.ones[:], 1.0)
-    f_et = fill(T.et[:], 0.0)
+    f_half = fill(T.half[:], 0.5)
     f_tb = fill(T.tb[:], 0.0)
-    f_dp = fill(T.dp[:], LOW)
-    ident = op("g", lambda: g.affine_select(T.ident[:], T.ones[:], [[-1, 128]], ALU.is_equal, 0.0, 0, 1), f_ones, grp="gs")
+    f_et = fill(T.et[:], 0.0)
+    ident = op("g", lambda: g.affine_select(T.ident[:], T.half[:], [[-1, 128]], ALU.is_equal, 0.0, 0, 1), f_half, grp="gs")
     op("g", lambda: g.iota(T.bas[:], [[-64, 8], [16, 4]], 128, 0, allow_small_or_imprecise_dtypes=True), grp="gs")
-    op("g", lambda: g.iota(T.dn[:], [[-1, 17]], 24, 0, allow_small_or_imprecise_dtypes=True), grp="gs")
+    tb0 = op("g", lambda: g.iota(T.tb[0:96, 1224:1530:2], [[-1, 17], [0, 9]], 16, 0, allow_small_or_imprecise_dtypes=True), f_tb)
 
     order = [r ^ 3, r ^ 1, r ^ 2, r] if even else [r ^ 1, r ^ 3, r, r ^ 2]
     cx = [cp("v" if k < 2 else "s", T.xt[:, 256 * k:256 * k + 256], T.xin[:, :, order[k], :], ldx, grp="px%d" % (k // 2)) for k in range(4)]
@@ -214,25 +219,24 @@ def rank_program(g, core, T, topo):
     ARRP, ARRO, SENT = ("arrp", 12), ("arro", 20), ("sent", 32)
     ldw = dma("g", T.win[:], T.w[:], SENT)
 
+    def sfill(ap, k, c):
+        return op("s", lambda: S.activation(ap, T.xin[:, :, :, 0:k], AF.Identity, bias=c, scale=0.0), ldx, grp="sf")
+
+    sfill(T.dp[:, 0:4], 54, LOW)
+    sfill(T.dp[:, 4:6], 27, LOW)
+    sfill(T.gr[:, 0:960], 60, 0.0)
+    sf = sfill(T.gr[:, 960:1920], 60, 0.0)
     st = fill(T.spr[0:32, :], 0.0, grp="st")
-    f_ab = fill(T.ab[:], 0.0)
-    f_rs = fill(T.rs[:], 1.0)
+    f_rs = fill(T.rs[:], 0.0)
     t_b = op("v", lambda: V.transpose(T.bt[:], T.bas[:]), ident)
     ce = [cp("v", T.et[:, 517 * k + 2:517 * k + 514:4], T.ident[:], ident, f_et) for k in range(2)]
     fill(T.mk[:], 1.0, grp="st")
-    fill(T.gr[:], 0.0, grp="st")
-    fill(T.dp[0:32, 0, 1:2], 0.0, f_dp, grp="st")
-    fill(T.sen[0:96, :], 25.0, grp="st")
+    fill(T.ones[:, 0:16], 1.0, grp="st")
+    fill(T.sen[0:96, :], 17.0, grp="st")
     fill(T.sen[96:128, :], 1.0, grp="st")
-    fill(T.rs[:, 0:136:34], 0.0, f_rs, grp="st")
-    fill(T.tb[0:96, 6:816:204], 25.0, f_tb, grp="st")
-    fill(T.tb[96:128, 6:816:204], 1.0, f_tb, grp="st")
-    cp("v", T.tb[0:96, 822:1014:12], T.dn[0:96, 0:16], f_tb, grp="st")
-    cp("v", T.tb[0:96, 826:1018:12], T.dn[0:96, 1:17], f_tb, grp="st")
-    op("v", lambda: V.tensor_scalar(T.ab[:, 1:136:34], T.bt[:, 0:4], -1.0, -16.0, ALU.mult, ALU.add), t_b, f_ab, grp="st")
+    op("v", lambda: V.tensor_scalar(T.rs[:, 0:68:17], T.bt[:, 0:4], 16.0, None, ALU.add), t_b, f_rs, tb0, grp="st")
     op("v", lambda: V.tensor_scalar(T.nb[:], T.bt[:, 0:1], -1.0, None, ALU.mult), t_b, grp="st")
-    op("v", lambda: V.tensor_scalar(T.pb[:], T.bt[:, 0:1], 16.0, None, ALU.add), t_b, grp="st")
-    cp("v", T.sm[0:32, 33:1088:544], T.bt[0:32, 0:2], t_b, grp="st")
+    cp("v", T.sm[0:32, 16:544:272], T.bt[0:32, 0:2], t_b, grp="st")
     for b in range(4):
         k = 516 * (b % 2) + 2 - 2 * (b // 2)
         q_e = quant(T.eq[:, 128 * b:128 * b + 128], T.eqs[:, 128 * b:128 * b + 128], T.et[:, k:k + 512], ce, grp="z")
@@ -243,6 +247,8 @@ def rank_program(g, core, T, topo):
 
     def zeros2():
         fill(T.t1[:, 256:512], 0.0, grp="zz")
+
+    def zeros3():
         zz.append(fill(T.tl[:, 256:512], 0.0, grp="zz"))
 
     zz = []
@@ -251,130 +257,122 @@ def rank_program(g, core, T, topo):
         return cp(q, T.spr[0:16, c:512:32], T["ps%d" % bank][32 * a:32 * a + 16, col:col + 16], *deps, grp=grp)
 
     def align(sp, lo, n, off, beside):
-        def turn(q):
-            return op("v", lambda: V.transpose(T.gr[quarter(q), 3:768:6], T.spr[0:32, 128 * q:128 * q + 128]), sp)
+        def turn(q, i0, i1):
+            s0 = i0 - 4 * q
+            return op("v", lambda: V.transpose(T.gr[quarter(q), 384 * s0:384 * (s0 + i1 - i0):12], T.spr[0:32, 32 * i0:32 * i1]), sp, sf)
 
-        def row(i, q, slot, second, *deps, grp=None):
-            a, b = divmod(i, 4)
-            step, m, at, g0 = (3, 32, (4, 0), 0) if i % 2 == 0 else (2, 48, (3, 2), 1)
-            k = at[second]
-            return scan(T.dp[quarter(q), slot, k:k + step * m - 1:step], T.dp[quarter(a), b, 1:step * m:step],
-                        T.gr[quarter(a), 192 * b + g0:192 * b + 96:step], LOW, ALU.max, ALU.add, *deps, grp=grp)
+        def row(i, q, slot, at, *deps, grp=None):
+            a = max(i - 1, 0) // 4
+            s0 = i - 4 * a
+            step = (6, 4, 3)[i % 3] if i else 4
+            return scan(T.dp[quarter(q), slot, 12 + at:204 + at:step], T.dp[quarter(a), s0, 12:204:step],
+                        T.gr[quarter(a), 384 * s0:384 * s0 + 192:step], LOW if i else 0.0, ALU.max, ALU.add, *deps, grp=grp)
+
+        def was(part, b, c):
+            return T.dp[part, b:c, 0:192:12], T.dp[part, b:c, 12:204:12]
 
         low, top, every = slice(0, 96), slice(96, 128), slice(0, 128)
 
-        def lfv(b, part):
-            return T.mk[part, b, 45::-3] if b % 2 else T.mk[part, b, 61::-4]
+        def best(b, c, part, *deps):
+            return tt(T.um[part, b:c, :], *was(part, b + 1, c + 1), ALU.max, *deps)
 
-        def best(b, part, *deps):
-            return tt(T.um[part, b, :], T.dp[part, b, 1:92:6], T.dp[part, b, 7:98:6], ALU.max, *deps)
+        def left(b, c, part, *deps):
+            return tt(T.mk[part, b:c, 142::-9], was(part, b + 2, c + 2)[0], T.um[part, b:c, :], ALU.is_gt, *deps)
 
-        def left(b, part, *deps):
-            return tt(lfv(b, part), T.dp[part, b + 1, 1:92:6], T.um[part, b, :], ALU.is_gt, *deps)
+        def diag(b, c, part, *deps):
+            return tt(T.dg[part, b:c, :], *was(part, b + 2, c + 2), ALU.is_ge, *deps)
 
-        def diag(b, part, *deps):
-            return tt(T.dg[part, b, :], T.dp[part, b + 1, 1:92:6], T.dp[part, b + 1, 7:98:6], ALU.is_ge, *deps)
+        def either(b, c, part, *deps):
+            return tt(T.mk[part, b:c, 143::-9], T.mk[part, b:c, 142::-9], T.dg[part, b:c, :], ALU.max, *deps)
 
-        def either(b, part, *deps):
-            z = T.mk[part, b, 46::-3] if b % 2 else T.mk[part, b, 62::-4]
-            return tt(z, lfv(b, part), T.dg[part, b, :], ALU.max, *deps)
+        def table(b, part, *deps):
+            k, m = 306 * b, 145 + 2 * b
+            return scan(T.tb[part, k:k + 2 * m:2], T.tb[part, k + 306:k + 306 + 2 * m:2], T.mk[part, b, 6 - 2 * b:151],
+                        T.sen[part, 0:1], ALU.max, ALU.mult, *deps)
 
-        tr = [turn(0)]
-        last, dup, um, lf, dg, z = st, [], {}, {}, {}, {}
+        tr = {0: turn(0, 0, 2)}
+        last, dup = st, []
         for i in range(16):
-            a, b = divmod(i, 4)
             prev, gr = last, group()
-            if i == 15:
-                last = [row(i, a, 4, 0, prev)]
-            elif b == 3:
-                last = [row(i, a + 1, 0, k, prev, grp=gr) for k in (0, 1)]
-                dup.append(row(i, a, 4, 0, prev))
+            ats = (0,) if i in (0, 15) else ((0, 8), (0, 9), (0,))[i % 3]
+            if i in (4, 8, 12):
+                last = [row(i, i // 4, 1, at, prev, grp=gr) for at in ats]
+                dup.append(row(i, i // 4 - 1, 5, 0, prev))
             else:
-                last = [row(i, a, b + 1, k, prev, tr[a], grp=gr) for k in (0, 1)]
-            if i < 3:
-                tr.append(turn(1 + i))
-            if i == 11:
-                um[3] = best(3, low, prev)
+                last = [row(i, i // 4, 1 + i % 4, at, prev, tr.get(i, []), grp=gr) for at in ats]
+            if i < 4:
+                tr[(2, 5, 9, 13)[i]] = turn(i, (2, 5, 9, 13)[i], (5, 9, 13, 16)[i])
             if i == 12:
-                lf[3], dg[3], um[0] = left(3, low, um[3], dup), diag(3, low, dup), best(0, every, prev)
+                ul = best(2, 4, low, prev)
             if i == 13:
-                z[3], um[1], dg[0] = either(3, low, lf[3], dg[3]), best(1, every, prev), diag(0, every, prev)
+                dl, ll = diag(2, 4, low, dup), left(2, 4, low, ul, dup)
             if i == 14:
-                um[2], lf[0], dg[1] = best(2, every, prev), left(0, every, um[0]), diag(1, every, prev)
+                ue, zl = best(0, 2, every, prev), either(2, 4, low, ll, dl)
             if i == 15:
-                u15, lf[2], dg[2] = best(3, top, prev), left(2, every, um[2], prev), diag(2, every, prev)
+                ut, le, de = best(2, 3, top, prev), left(0, 2, every, ue, prev), diag(0, 2, every, prev)
             if i in beside:
                 beside[i]()
 
-        def table(b, second, *deps, grp=None):
-            k = 204 * b
-            if b % 2:
-                step, m, at, x, mask = 4, 48, (10, 1), 2, T.mk[:, b, 0:48]
-            else:
-                step, m, at, x, mask = 3, 64, (9, 1), 0, T.mk[:, b, 0:64]
-            o = k + at[second]
-            return scan(T.tb[:, o:o + step * m - 2:step], T.tb[:, k + 204 + x:k + 204 + x + step * m - 2:step], mask,
-                        T.sen[:, 0:1], ALU.max, ALU.mult, *deps, grp=grp)
-
-        last = left(3, top, last, u15)
-        z[2], lf[1] = either(2, every, lf[2], dg[2]), left(1, every, um[1])
-        for b in (3, 2, 1, 0):
-            prev, gr = last, group()
-            last = [table(b, k, prev, z[b], grp=gr) for k in ((0, 1) if b else (0,))]
-            if b == 3:
-                z[1], z[0] = either(1, every, lf[1], dg[1]), either(0, every, lf[0], dg[0])
+        last = left(2, 3, top, last, ut)
+        tl, ze = table(3, low, zl), either(0, 2, every, le, de)
+        for b in (2, 1, 0):
+            last = table(b, top, last, ze if b < 2 else [])
+            tl = table(b, low, tl, ze if b < 2 else [])
 
         gs = group()
 
         def seg(a, *deps):
-            f = 0 if a else 34
-            return [scan(T.sm[0:32, k + 136 * a + f:k + 136 * a + 136], T.rs[quarter(a), f:136], T.ab[quarter(a), f:136],
-                         0.0, ALU.mult, ALU.subtract, *deps, grp=gs) for k in (0, 544)]
+            m, flags = (68, T.ab[quarter(a), :]) if a < 3 else (51, T.tb[top, 0:918:18])
+            return [scan(T.sm[0:32, k + 68 * a + 17:k + 68 * a + 17 + m], T.rs[quarter(a), 0:m], flags,
+                         0.0, ALU.max, ALU.subtract, *deps, grp=gs) for k in (0, 272)]
 
         def cmp(a, c, e, *deps):
             q = quarter(a)
-            return op("v", lambda: V.tensor_scalar(T.ab[q, 0:136:2], T.tb[q, 6:816:12], c, e, ALU.mult, ALU.is_gt), *deps)
+            return op("v", lambda: V.tensor_scalar(T.ab[q, :], T.tb[q, 0:1224:18], c, e, ALU.mult, ALU.is_gt), *deps)
 
         def look(a, c, e, *deps):
-            return op("s", lambda: S.activation(T.sgn[quarter(a - 1), :], T.tb[quarter(a), 6:199:4], AF.Sign, bias=e, scale=c,
+            return op("s", lambda: S.activation(T.sgn[quarter(a - 1), :], T.tb[quarter(a), 0:289:9], AF.Sign, bias=e, scale=c,
                                                 accum_out=T.ev[quarter(a - 1), :]), *deps)
 
-        e2, e1, e0 = T.e2[64:96, 16:17], T.ev[32:64, :], T.ev[0:32, :]
-        j12 = scan(T.e2[64:96, :], T.ones[96:128, 0:17], T.tb[96:128, 6:210:12], 24.5, ALU.mult, ALU.subtract, last)
-        s3 = scan(T.en[64:96, :], T.rs[96:128, 0:136:2], T.tb[96:128, 6:816:12], 0.0, ALU.mult, ALU.subtract, last)
-        j8 = look(2, -1.0, e2, j12)
-        cs, gc = [], group()
-        for k in (0, 544):
-            cs.append(op("s", lambda k=k: S.activation(T.sm[0:32, k + 441:k + 544:34], T.en[64:96, 16:68:17],
-                                                       AF.Identity, bias=T.pb[64:96, :]), s3, st, grp=gc))
-        j4 = look(1, -2.0, e1, j8)
-        c2 = cmp(2, 1.0, e2, j12)
-        c1 = cmp(1, 2.0, e1, j8)
+        e2, e1, e0 = T.e2[64:96, 15:16], T.ev[32:64, :], T.ev[0:32, :]
+        j13 = scan(T.e2[64:96, :], T.ones[96:128, 0:16], T.tb[96:128, 18:306:18], 15.5, ALU.mult, ALU.subtract, last)
+        seg(3, last)
+        j9 = look(2, -1.0, e2, j13, tl)
+        j5 = look(1, -2.0, e1, j9)
+        c2 = cmp(2, 1.0, e2, j13, tl)
+        c1 = cmp(1, 2.0, e1, j9)
         seg(2, c2)
-        c0 = cmp(0, 2.0, e0, j4)
+        c0 = cmp(0, 2.0, e0, j5)
         seg(1, c1)
         s0 = seg(0, c0)
-        tj = op("v", lambda: V.transpose(T.jt[0:32, :], T.sm[0:32, 33:1088:34]), s0, cs)
-        gl = group()
-        return [cp("v", off[quarter(a), :], T.jt[0:32, lo:lo + n], tj, grp=gl) for a in range(4)], [s0, cs], tj
+        gj, gl = group(), group()
+        tj = [op("v", lambda a=a: V.transpose(T.jt[quarter(a), :], T.sm[0:32, 16:544:17]), s0, grp=gj) for a in (0, 1)]
+        return [cp("v", off[64 * a:64 * a + 64, :], T.jt[0:64, lo:lo + n], tj, grp=gl) for a in (0, 1)], s0, tj
 
     def unpack(hf, n, x, xs, at, *deps):
         gu = group()
         out = []
         for b in range(4):
             m = mm(4 + b, n, T.eq, T.eqs, 128 * b, x, xs, at, *deps)
-            out.append(op("s", lambda b=b: S.activation(hf[:, n * b:n * b + n], T["ps%d" % (4 + b)][:, 0:n], AF.Copy, scale=0.5), m, grp=gu))
+            out.append(cp("s", hf[:, n * b:n * b + n], T["ps%d" % (4 + b)][:, 0:n], m, grp=gu))
         return out
 
     def blend(tile, n, hf, w, a, b0, b1, off, bs, *deps, grp=None):
         return [tt(tile[:, b:4 * n:4], hf[:, w * b + b0:w * b + b1].indirect(off), hf[:, w * b + a:w * b + a + n], ALU.add, *deps, grp=grp)
                 for b in bs]
 
+    def blend2(tile, n, hf, w, a, b0, b1, off, k, pk, *deps):
+        gb = group()
+        got = [cp("s", pk[:, n * (b - k):n * (b - k + 1)], hf[:, w * b + b0:w * b + b1].indirect(off), *deps) for b in range(k, 4)]
+        out = blend(tile, n, hf, w, a, b0, b1, off, range(k), *deps, grp=gb)
+        return out + [tt(tile[:, b:4 * n:4], pk[:, n * (b - k):n * (b - k + 1)], T["ps%d" % (4 + b)][:, a:a + n], ALU.add, got[b - k], grp=gb)
+                      for b in range(k, 4)]
+
     L, LS = T.lnd, T.lnds
     w0 = mm(0, 128, L, LS, BO, L, LS, AO, q_o, ARRP)
     w1 = mm(1, 128, L, LS, BO + 16, L, LS, AO)
-    w2 = mm(2, 128, L, LS, BX, L, LS, AO + 64, ARRO)
-    w3 = mm(3, 128, L, LS, BX + 16, L, LS, AO + 64)
+    w3 = mm(3, 128, L, LS, BX + 16, L, LS, AO + 64, ARRO)
+    w2 = mm(2, 128, L, LS, BX, L, LS, AO + 64)
     sp0 = {0: [], 1: [], 2: [], 3: []}
     for c in range(12):
         bcol = 128 + 16 * c - 128 * (c // 4)
@@ -384,8 +382,8 @@ def rank_program(g, core, T, topo):
             bank, a, col = 2 + (bcol // 16) % 2, bcol // 32, 16 * c - 64
         sp0[bank].append(spread("v" if bank % 2 == 0 else "s", bank, a, col, c, [w0, w1, w2, w3][bank], st, grp="sp%d" % (bank % 2)))
     u0 = unpack(T.hf0, 384, L, LS, BX, q_e)
-    lst0, _, tj0 = align([sp0[k] for k in range(4)], 0, 12, T.off0, {4: zeros, 5: zeros2})
-    h0 = blend(T.t0, 128, T.hf0, 384, 256, 0, 192, T.off0[:, 4:12], range(4), lst0, u0, grp=group())
+    lst0, _, tj0 = align([sp0[k] for k in range(4)], 0, 12, T.off0, {5: zeros, 6: zeros2, 7: zeros3})
+    h0 = blend2(T.t0, 128, T.hf0, 384, 256, 0, 192, T.off0[:, 4:12], 2, T.pk0, lst0, u0)
     par = r >> 1
     ju = [tt(T.ju[0:32, par:8:2], T.jt[0:32, 4:8], T.bas[0:32, 4:8], ALU.subtract, tj0),
           tt(T.ju[0:32, 1 - par:8:2], T.jt[0:32, 0:4], T.bas[0:32, 0:4], ALU.subtract, tj0)]
@@ -402,8 +400,8 @@ def rank_program(g, core, T, topo):
     quant_w()
 
     Q, QS = T.q0, T.q0s
-    wa = mm(0, 128, Q, QS, 0, Q, QS, 0, q0, sp0[0])
-    wb = mm(1, 128, Q, QS, 16, Q, QS, 0, sp0[1])
+    wb = mm(1, 128, Q, QS, 16, Q, QS, 0, q0, sp0[1])
+    wa = mm(0, 128, Q, QS, 0, Q, QS, 0, sp0[0])
     sp1 = [spread("v" if k % 2 == 0 else "s", k % 2, bb // 32 + k // 2, ab + 16 * k, 8 + k, [wa, wb][k % 2], grp="sq%d" % (k % 2)) for k in range(4)]
     u1 = unpack(T.hf1, 128, Q, QS, 0, u0)
     cy0, hl = [], []
@@ -424,10 +422,10 @@ def rank_program(g, core, T, topo):
             cy0.append(cp("s", T.ys0[:, o, 1 - par:8:2, :], T["ps%d" % bank][:, 0:64], m))
             dma("y", T.y[:, 192 * o:192 * o + 128], T.ys0[:, o], cy0[o], cy0[3 + o], grp="oy")
 
-    lst1, sm1, _ = align(sp1, 8, 4, T.off1, {4: y_own, 5: rest, 6: rest, 8: rest, 9: rest, 10: y_rest})
-    p1 = op("s", lambda: S.activation(T.pj1[0:32, :], T.sm[0:32, 33:544:34], AF.Identity, bias=T.nb[0:32, :]), sm1)
+    lst1, sm1, _ = align(sp1, 8, 4, T.off1, {5: rest, 6: rest, 7: rest, 9: rest, 10: y_own, 11: y_rest})
+    h1 = blend2(T.t1, 64, T.hf1, 128, ab, bb, bb + 64, T.off1[:], 3, T.pk1, lst1, u1)
+    p1 = op("s", lambda: S.activation(T.pj1[0:32, :], T.sm[0:32, 16:272:17], AF.Identity, bias=T.nb[0:32, :]), sm1)
     og = dma("g", T.pt[0:1, 128:192], T.pj1[8:12, :], p1, grp="og")
-    h1 = blend(T.t1, 64, T.hf1, 128, ab, bb, bb + 64, T.off1[:], range(4), lst1, u1, grp=group())
     q1 = quant(T.q1[:], T.q1s[:], T.t1[:], h1, zz)
     my = [mm(1 + o, 128, T.wq, T.wqs, 128 * o, T.q1, T.q1s, 0, q1, cy0, sp1) for o in range(3)]
     dma("y", T.oc[:], u8(T.q1[:, 0:64]), q1, grp="oy")

from concourse.bass import DstId, RemoteDMATransfer
from concourse.mybir import dt, AluOpType, ActivationFunctionType

ALU = AluOpType
AF = ActivationFunctionType
X4, U8, F32, BF = "float8_e4m3fn_x4", "uint8", "float32", "bfloat16"
LOW = -1e29

SCRATCH = {
    "xin": ("sbuf", [128, 4, 4, 64], BF),
    "xt": ("sbuf", [128, 1024], BF),
    "snd": ("sbuf", [128, 128], X4), "snds": ("sbuf", [128, 128], U8),
    "lnd": ("sbuf", [128, 512], X4), "lnds": ("sbuf", [128, 512], U8),
    "win": ("sbuf", [128, 1536], BF),
    "wq": ("sbuf", [128, 384], X4), "wqs": ("sbuf", [128, 384], U8),
    "ones": ("sbuf", [128, 128], BF), "half": ("sbuf", [128, 128], BF), "ident": ("sbuf", [128, 128], BF),
    "et": ("sbuf", [128, 1032], BF),
    "eq": ("sbuf", [128, 512], X4), "eqs": ("sbuf", [128, 512], U8),
    "bas": ("sbuf", [128, 32], F32), "bt": ("sbuf", [128, 32], F32),
    "nb": ("sbuf", [128, 1], F32),
    "sen": ("sbuf", [128, 2], BF), "rs": ("sbuf", [128, 68], BF),
    "spr": ("sbuf", [128, 512], F32),
    "gr": ("sbuf", [128, 1920], F32),
    "dp": ("sbuf", [128, 6, 216], F32),
    "um": ("sbuf", [128, 4, 16], F32),
    "dg": ("sbuf", [128, 4, 16], BF), "mk": ("sbuf", [128, 4, 160], BF),
    "tb": ("sbuf", [128, 1536], BF),
    "ab": ("sbuf", [128, 68], BF),
    "sm": ("sbuf", [128, 544], F32),
    "e2": ("sbuf", [128, 16], F32), "ev": ("sbuf", [128, 1], F32), "sgn": ("sbuf", [128, 33], F32),
    "jt": ("sbuf", [128, 32], F32), "ju": ("sbuf", [128, 32], F32), "jv": ("sbuf", [128, 32], F32),
    "off0": ("sbuf", [128, 12], "uint16"), "off1": ("sbuf", [128, 4], "uint16"),
    "pj1": ("sbuf", [128, 16], F32),
    "hf0": ("sbuf", [128, 1536], F32), "hf1": ("sbuf", [128, 512], F32),
    "pk0": ("sbuf", [128, 256], F32), "pk1": ("sbuf", [128, 64], F32),
    "t0": ("sbuf", [128, 576], BF), "tl": ("sbuf", [128, 512], BF), "t1": ("sbuf", [128, 512], BF),
    "q0": ("sbuf", [128, 144], X4), "q0s": ("sbuf", [128, 144], U8),
    "ql": ("sbuf", [128, 128], X4), "qls": ("sbuf", [128, 128], U8),
    "q1": ("sbuf", [128, 128], X4), "q1s": ("sbuf", [128, 128], U8),
    "ys0": ("sbuf", [128, 3, 8, 16], F32), "ys1": ("sbuf", [128, 192], F32),
}
for _k in range(8):
    SCRATCH["ps%d" % _k] = ("psum", [128, 512], F32)

NSEM = 140
SEMAPHORES = ["arrp", "arro", "sent"] + ["s%d" % _k for _k in range(NSEM)]


def _emit(ops, queues, T):
    n = len(ops)
    members = {}
    for i, o in enumerate(ops):
        if o["grp"]:
            members.setdefault(o["grp"], []).append(i)
    known = {q: set() for q in queues}
    before = [None] * n
    waiters = {}
    for i, o in enumerate(ops):
        k = known[o["q"]]
        w = []
        ext = [d for d in o["deps"] if isinstance(d, tuple)]
        own = sorted(set(d for d in o["deps"] if not isinstance(d, tuple)), reverse=True)
        for d in ext:
            if d not in k:
                k.add(d)
                w.append(d)
        for d in own:
            if d in k:
                continue
            for m in (members[ops[d]["grp"]] if ops[d]["grp"] else [d]):
                k.add(m)
                k |= before[m]
            w.append(d)
            waiters.setdefault(ops[d]["grp"] or d, set()).add(o["q"])
        o["waits"] = w
        before[i] = set(k)
    nxt = [0]

    def fresh():
        nxt[0] += 1
        return "s%d" % (nxt[0] - 1)

    final = {}
    for i, o in enumerate(ops):
        for d in o["waits"]:
            if not isinstance(d, tuple):
                final[ops[d]["grp"] or d] = i
    pools = {q: [] for q in queues}
    sem, total = {}, {}
    for i, o in enumerate(ops):
        key = o["grp"] or i
        if key in waiters and key not in sem:
            if (not o["grp"] or o["grp"][0] == "p") and o["inc"] == 1 and waiters[key] == {o["q"]}:
                p = [e for e in pools[o["q"]] if e[1] <= i]
                if not p:
                    p = [[fresh(), 0]]
                    pools[o["q"]].append(p[0])
                sem[key] = p[0][0]
                p[0][1] = final[key]
            else:
                sem[key] = fresh()
                total[key] = sum(ops[m]["inc"] for m in members[key]) if o["grp"] else o["inc"]
    count = {}
    for i, o in enumerate(ops):
        e = queues[o["q"]]
        for d in o["waits"]:
            if isinstance(d, tuple):
                e.wait_ge(T.sem[d[0]], d[1])
            else:
                key = ops[d]["grp"] or d
                e.wait_ge(T.sem[sem[key]], total[key] if key in total else count[sem[key]])
        if o["fn"] is None:
            continue
        ins = o["fn"]()
        key = o["grp"] or i
        if key in sem:
            ins.then_inc(T.sem[sem[key]], o["inc"])
            count[sem[key]] = count.get(sem[key], 0) + o["inc"]


def rank_program(g, core, T, topo):
    r = T.rank_of(core)
    if r is None:
        return
    V, S, P, Y = g.vector, g.scalar, g.tensor, g.sync
    ops = []
    serial = [0]

    def flat(ds):
        out = []
        for d in ds:
            if isinstance(d, list):
                out += flat(d)
            else:
                out.append(d)
        return out

    def op(q, fn, *deps, grp=None, inc=1):
        ops.append({"q": q, "fn": fn, "deps": flat(deps), "grp": grp, "inc": inc})
        return len(ops) - 1

    def dma(q, out, in_, *deps, grp=None):
        e = {"g": g, "y": Y, "s": S}[q]
        return op(q, lambda: e.dma_start(out, in_), *deps, grp=grp, inc=16)

    def fill(ap, c, *deps, grp=None):
        return op("v", lambda: V.memset(ap, c), *deps, grp=grp)

    def cp(q, out, in_, *deps, grp=None):
        if q == "v":
            return op("v", lambda: V.tensor_copy(out, in_), *deps, grp=grp)
        return op("s", lambda: S.activation(out, in_, AF.Copy), *deps, grp=grp)

    def quant(out, sc, in_, *deps, grp=None):
        return op("v", lambda: V.quantize_mx(out, sc, in_), *deps, grp=grp)

    def mm(bank, n, w, ws, a, x, xs, b, *deps):
        return op("p", lambda: P.matmul_mx(T["ps%d" % bank][:, 0:n], w[:, a:a + 128], ws[:, a:a + 128],
                                           x[:, b:b + n], xs[:, b:b + n], True, True), *deps)

    def tt(out, a, b, o, *deps, grp=None):
        return op("v", lambda: V.tensor_tensor(out, a, b, o), *deps, grp=grp)

    def scan(out, a, b, init, o0, o1, *deps, grp=None):
        return op("v", lambda: V.tensor_tensor_scan(out, a, b, init, o0, o1), *deps, grp=grp)

    def quarter(a):
        return slice(32 * a, 32 * a + 32)

    def group():
        serial[0] += 1
        return "p%d" % serial[0]

    BX, BO, AO, AX = 64, 128, 256, 384
    even = r % 2 == 0
    own = AO if even else BO
    ab, bb = (0, 64) if r < 2 else (64, 0)

    ldx = dma("y", T.xin[:], T.x[:])
    f_half = fill(T.half[:], 0.5)
    f_tb = fill(T.tb[:], 0.0)
    f_et = fill(T.et[:], 0.0)
    ident = op("g", lambda: g.affine_select(T.ident[:], T.half[:], [[-1, 128]], ALU.is_equal, 0.0, 0, 1), f_half, grp="gs")
    op("g", lambda: g.iota(T.bas[:], [[-64, 8], [16, 4]], 128, 0, allow_small_or_imprecise_dtypes=True), grp="gs")
    tb0 = op("g", lambda: g.iota(T.tb[0:96, 1224:1530:2], [[-1, 17], [0, 9]], 16, 0, allow_small_or_imprecise_dtypes=True), f_tb)

    order = [r ^ 3, r ^ 1, r ^ 2, r] if even else [r ^ 1, r ^ 3, r, r ^ 2]
    cx = [cp("v" if k < 2 else "s", T.xt[:, 256 * k:256 * k + 256], T.xin[:, :, order[k], :], ldx, grp="px%d" % (k // 2)) for k in range(4)]
    q_s = quant(T.snd[:], T.snds[:], T.xt[:, 0:512], cx[0])
    q_o = quant(T.lnd[:, own:own + 128], T.lnds[:, own:own + 128], T.xt[:, 512:1024], cx[2])

    def u8(v):
        return v.bitcast(dt.uint8)

    def bits(es):
        return sum(1 << e for e in es)

    peer = {k: T.cores[r ^ k] for k in (1, 2, 3)}
    e1, e3 = topo.engines(core, peer[1]), topo.engines(core, peer[3])
    far = [e for e in e1 if e in e3][:8]
    near = [e for e in topo.engines(core, peer[2]) if e not in far][::2][:4]

    def xfer(k, es, sem, src, dst):
        a = topo.addr(peer[k])
        return RemoteDMATransfer(dst_ids=[DstId(rid=a[0], pnc=a[1])], dma_engine_mask=bits(es), remote_sem=T.sem[sem], src=src, dst=dst)

    h = 0 if even else 64
    dc = AX if even else BX
    dsc = dc - h
    a1 = topo.addr(peer[1])
    op("g", lambda: g.remote_dma(u8(T.lnd[:, own:own + 128]), u8(T.snd[:]), T.sem.arrp, T.sem.sent, a1[1], a1[0], bits(far)), q_s)
    op("g", lambda: g.remote_dma_fused([
        xfer(1, far[:4], "arrp", T.snds[:], T.lnds[:, own:own + 128]),
        xfer(3, far[4:], "arro", T.snds[:], T.lnds[:, dsc:dsc + 128]),
        xfer(2, near, "arro", T.lnds[:, own:own + 128], T.lnds[:, dsc:dsc + 128])], local_sem=T.sem.sent), q_o)
    op("g", lambda: g.remote_dma_fused([
        xfer(3, far, "arro", u8(T.snd[:, h:h + 64]), u8(T.lnd[:, dc:dc + 64])),
        xfer(2, near, "arro", u8(T.lnd[:, own + h:own + h + 64]), u8(T.lnd[:, dc:dc + 64]))], local_sem=T.sem.sent))
    ARRP, ARRO, SENT = ("arrp", 12), ("arro", 20), ("sent", 32)
    ldw = dma("g", T.win[:], T.w[:], SENT)

    def sfill(ap, k, c):
        return op("s", lambda: S.activation(ap, T.xin[:, :, :, 0:k], AF.Identity, bias=c, scale=0.0), ldx, grp="sf")

    sfill(T.dp[:, 0:4], 54, LOW)
    sfill(T.dp[:, 4:6], 27, LOW)
    sfill(T.gr[:, 0:960], 60, 0.0)
    sf = sfill(T.gr[:, 960:1920], 60, 0.0)
    st = fill(T.spr[0:32, :], 0.0, grp="st")
    f_rs = fill(T.rs[:], 0.0)
    t_b = op("v", lambda: V.transpose(T.bt[:], T.bas[:]), ident)
    ce = [cp("v", T.et[:, 517 * k + 2:517 * k + 514:4], T.ident[:], ident, f_et) for k in range(2)]
    fill(T.mk[:], 1.0, grp="st")
    fill(T.ones[:, 0:16], 1.0, grp="st")
    fill(T.sen[0:96, :], 17.0, grp="st")
    fill(T.sen[96:128, :], 1.0, grp="st")
    op("v", lambda: V.tensor_scalar(T.rs[:, 0:68:17], T.bt[:, 0:4], 16.0, None, ALU.add), t_b, f_rs, tb0, grp="st")
    op("v", lambda: V.tensor_scalar(T.nb[:], T.bt[:, 0:1], -1.0, None, ALU.mult), t_b, grp="st")
    cp("v", T.sm[0:32, 16:544:272], T.bt[0:32, 0:2], t_b, grp="st")
    for b in range(4):
        k = 516 * (b % 2) + 2 - 2 * (b // 2)
        q_e = quant(T.eq[:, 128 * b:128 * b + 128], T.eqs[:, 128 * b:128 * b + 128], T.et[:, k:k + 512], ce, grp="z")

    def zeros():
        fill(T.t0[:, 512:576], 0.0, grp="zz")
        fill(T.ju[0:32, 8:32], 0.0, grp="zz")

    def zeros2():
        fill(T.t1[:, 256:512], 0.0, grp="zz")

    def zeros3():
        zz.append(fill(T.tl[:, 256:512], 0.0, grp="zz"))

    zz = []

    def spread(q, bank, a, col, c, *deps, grp=None):
        return cp(q, T.spr[0:16, c:512:32], T["ps%d" % bank][32 * a:32 * a + 16, col:col + 16], *deps, grp=grp)

    def align(sp, lo, n, off, beside):
        def turn(q, i0, i1):
            s0 = i0 - 4 * q
            return op("v", lambda: V.transpose(T.gr[quarter(q), 384 * s0:384 * (s0 + i1 - i0):12], T.spr[0:32, 32 * i0:32 * i1]), sp, sf)

        def row(i, q, slot, at, *deps, grp=None):
            a = max(i - 1, 0) // 4
            s0 = i - 4 * a
            step = (6, 4, 3)[i % 3] if i else 4
            return scan(T.dp[quarter(q), slot, 12 + at:204 + at:step], T.dp[quarter(a), s0, 12:204:step],
                        T.gr[quarter(a), 384 * s0:384 * s0 + 192:step], LOW if i else 0.0, ALU.max, ALU.add, *deps, grp=grp)

        def was(part, b, c):
            return T.dp[part, b:c, 0:192:12], T.dp[part, b:c, 12:204:12]

        low, top, every = slice(0, 96), slice(96, 128), slice(0, 128)

        def best(b, c, part, *deps):
            return tt(T.um[part, b:c, :], *was(part, b + 1, c + 1), ALU.max, *deps)

        def left(b, c, part, *deps):
            return tt(T.mk[part, b:c, 142::-9], was(part, b + 2, c + 2)[0], T.um[part, b:c, :], ALU.is_gt, *deps)

        def diag(b, c, part, *deps):
            return tt(T.dg[part, b:c, :], *was(part, b + 2, c + 2), ALU.is_ge, *deps)

        def either(b, c, part, *deps):
            return tt(T.mk[part, b:c, 143::-9], T.mk[part, b:c, 142::-9], T.dg[part, b:c, :], ALU.max, *deps)

        def table(b, part, *deps):
            k, m = 306 * b, 145 + 2 * b
            return scan(T.tb[part, k:k + 2 * m:2], T.tb[part, k + 306:k + 306 + 2 * m:2], T.mk[part, b, 6 - 2 * b:151],
                        T.sen[part, 0:1], ALU.max, ALU.mult, *deps)

        tr = {0: turn(0, 0, 2)}
        last, dup = st, []
        for i in range(16):
            prev, gr = last, group()
            ats = (0,) if i in (0, 15) else ((0, 8), (0, 9), (0,))[i % 3]
            if i in (4, 8, 12):
                last = [row(i, i // 4, 1, at, prev, grp=gr) for at in ats]
                dup.append(row(i, i // 4 - 1, 5, 0, prev))
            else:
                last = [row(i, i // 4, 1 + i % 4, at, prev, tr.get(i, []), grp=gr) for at in ats]
            if i < 4:
                tr[(2, 5, 9, 13)[i]] = turn(i, (2, 5, 9, 13)[i], (5, 9, 13, 16)[i])
            if i == 12:
                ul = best(2, 4, low, prev)
            if i == 13:
                dl, ll = diag(2, 4, low, dup), left(2, 4, low, ul, dup)
            if i == 14:
                ue, zl = best(0, 2, every, prev), either(2, 4, low, ll, dl)
            if i == 15:
                ut, le, de = best(2, 3, top, prev), left(0, 2, every, ue, prev), diag(0, 2, every, prev)
            if i in beside:
                beside[i]()

        last = left(2, 3, top, last, ut)
        tl, ze = table(3, low, zl), either(0, 2, every, le, de)
        for b in (2, 1, 0):
            last = table(b, top, last, ze if b < 2 else [])
            tl = table(b, low, tl, ze if b < 2 else [])

        gs = group()

        def seg(a, *deps):
            m, flags = (68, T.ab[quarter(a), :]) if a < 3 else (51, T.tb[top, 0:918:18])
            return [scan(T.sm[0:32, k + 68 * a + 17:k + 68 * a + 17 + m], T.rs[quarter(a), 0:m], flags,
                         0.0, ALU.max, ALU.subtract, *deps, grp=gs) for k in (0, 272)]

        def cmp(a, c, e, *deps):
            q = quarter(a)
            return op("v", lambda: V.tensor_scalar(T.ab[q, :], T.tb[q, 0:1224:18], c, e, ALU.mult, ALU.is_gt), *deps)

        def look(a, c, e, *deps):
            return op("s", lambda: S.activation(T.sgn[quarter(a - 1), :], T.tb[quarter(a), 0:289:9], AF.Sign, bias=e, scale=c,
                                                accum_out=T.ev[quarter(a - 1), :]), *deps)

        e2, e1, e0 = T.e2[64:96, 15:16], T.ev[32:64, :], T.ev[0:32, :]
        j13 = scan(T.e2[64:96, :], T.ones[96:128, 0:16], T.tb[96:128, 18:306:18], 15.5, ALU.mult, ALU.subtract, last)
        seg(3, last)
        j9 = look(2, -1.0, e2, j13, tl)
        j5 = look(1, -2.0, e1, j9)
        c2 = cmp(2, 1.0, e2, j13, tl)
        c1 = cmp(1, 2.0, e1, j9)
        seg(2, c2)
        c0 = cmp(0, 2.0, e0, j5)
        seg(1, c1)
        s0 = seg(0, c0)
        gj, gl = group(), group()
        tj = [op("v", lambda a=a: V.transpose(T.jt[quarter(a), :], T.sm[0:32, 16:544:17]), s0, grp=gj) for a in (0, 1)]
        return [cp("v", off[64 * a:64 * a + 64, :], T.jt[0:64, lo:lo + n], tj, grp=gl) for a in (0, 1)], s0, tj

    def unpack(hf, n, x, xs, at, *deps):
        gu = group()
        out = []
        for b in range(4):
            m = mm(4 + b, n, T.eq, T.eqs, 128 * b, x, xs, at, *deps)
            out.append(cp("s", hf[:, n * b:n * b + n], T["ps%d" % (4 + b)][:, 0:n], m, grp=gu))
        return out

    def blend(tile, n, hf, w, a, b0, b1, off, bs, *deps, grp=None):
        return [tt(tile[:, b:4 * n:4], hf[:, w * b + b0:w * b + b1].indirect(off), hf[:, w * b + a:w * b + a + n], ALU.add, *deps, grp=grp)
                for b in bs]

    def blend2(tile, n, hf, w, a, b0, b1, off, k, pk, *deps):
        gb = group()
        got = [cp("s", pk[:, n * (b - k):n * (b - k + 1)], hf[:, w * b + b0:w * b + b1].indirect(off), *deps) for b in range(k, 4)]
        out = blend(tile, n, hf, w, a, b0, b1, off, range(k), *deps, grp=gb)
        return out + [tt(tile[:, b:4 * n:4], pk[:, n * (b - k):n * (b - k + 1)], T["ps%d" % (4 + b)][:, a:a + n], ALU.add, got[b - k], grp=gb)
                      for b in range(k, 4)]

    L, LS = T.lnd, T.lnds
    w0 = mm(0, 128, L, LS, BO, L, LS, AO, q_o, ARRP)
    w1 = mm(1, 128, L, LS, BO + 16, L, LS, AO)
    w3 = mm(3, 128, L, LS, BX + 16, L, LS, AO + 64, ARRO)
    w2 = mm(2, 128, L, LS, BX, L, LS, AO + 64)
    sp0 = {0: [], 1: [], 2: [], 3: []}
    for c in range(12):
        bcol = 128 + 16 * c - 128 * (c // 4)
        if c < 8:
            bank, a, col = (bcol // 16) % 2, (bcol - 64) // 32, 16 * c
        else:
            bank, a, col = 2 + (bcol // 16) % 2, bcol // 32, 16 * c - 64
        sp0[bank].append(spread("v" if bank % 2 == 0 else "s", bank, a, col, c, [w0, w1, w2, w3][bank], st, grp="sp%d" % (bank % 2)))
    u0 = unpack(T.hf0, 384, L, LS, BX, q_e)
    lst0, _, tj0 = align([sp0[k] for k in range(4)], 0, 12, T.off0, {5: zeros, 6: zeros2, 7: zeros3})
    h0 = blend2(T.t0, 128, T.hf0, 384, 256, 0, 192, T.off0[:, 4:12], 2, T.pk0, lst0, u0)
    par = r >> 1
    ju = [tt(T.ju[0:32, par:8:2], T.jt[0:32, 4:8], T.bas[0:32, 4:8], ALU.subtract, tj0),
          tt(T.ju[0:32, 1 - par:8:2], T.jt[0:32, 0:4], T.bas[0:32, 0:4], ALU.subtract, tj0)]
    q0 = quant(T.q0[:], T.q0s[:], T.t0[:], h0, zz)
    jv = op("v", lambda: V.transpose(T.jv[0:32, :], T.ju[0:32, :]), ju, zz)
    oy = dma("y", T.pt[0:1, 0:128], T.jv[0:8, 0:16], jv, grp="oy")
    qw = []

    def quant_w():
        o = len(qw)
        qw.append(quant(T.wq[:, 128 * o:128 * o + 128], T.wqs[:, 128 * o:128 * o + 128], T.win[:, 512 * o:512 * o + 512], ldw))

    quant_w()
    quant_w()

    Q, QS = T.q0, T.q0s
    wb = mm(1, 128, Q, QS, 16, Q, QS, 0, q0, sp0[1])
    wa = mm(0, 128, Q, QS, 0, Q, QS, 0, sp0[0])
    sp1 = [spread("v" if k % 2 == 0 else "s", k % 2, bb // 32 + k // 2, ab + 16 * k, 8 + k, [wa, wb][k % 2], grp="sq%d" % (k % 2)) for k in range(4)]
    u1 = unpack(T.hf1, 128, Q, QS, 0, u0)
    cy0, hl = [], []

    def y_own():
        quant_w()
        for o, bank in enumerate((2, 3, 0)):
            m = mm(bank, 128, T.wq, T.wqs, 128 * o, Q, QS, 0, qw[o], sp0[2], sp0[3], sp1 if bank == 0 else [])
            cy0.append(cp("s", T.ys0[:, o, par:8:2, :], T["ps%d" % bank][:, 0:64], m))

    def rest():
        hl.append(blend(T.tl, 64, T.hf0, 384, 192, 0, 192, T.off0[:, 0:4], [len(hl)], lst0, u0))

    def y_rest():
        ql = quant(T.ql[:], T.qls[:], T.tl[:], hl, zz)
        for o, bank in enumerate((2, 3, 0)):
            m = mm(bank, 128, T.wq, T.wqs, 128 * o, T.ql, T.qls, 0, ql, cy0[o])
            cy0.append(cp("s", T.ys0[:, o, 1 - par:8:2, :], T["ps%d" % bank][:, 0:64], m))
            dma("y", T.y[:, 192 * o:192 * o + 128], T.ys0[:, o], cy0[o], cy0[3 + o], grp="oy")

    lst1, sm1, _ = align(sp1, 8, 4, T.off1, {5: rest, 6: rest, 7: rest, 9: rest, 10: y_own, 11: y_rest})
    h1 = blend2(T.t1, 64, T.hf1, 128, ab, bb, bb + 64, T.off1[:], 3, T.pk1, lst1, u1)
    p1 = op("s", lambda: S.activation(T.pj1[0:32, :], T.sm[0:32, 16:272:17], AF.Identity, bias=T.nb[0:32, :]), sm1)
    og = dma("g", T.pt[0:1, 128:192], T.pj1[8:12, :], p1, grp="og")
    q1 = quant(T.q1[:], T.q1s[:], T.t1[:], h1, zz)
    my = [mm(1 + o, 128, T.wq, T.wqs, 128 * o, T.q1, T.q1s, 0, q1, cy0, sp1) for o in range(3)]
    dma("y", T.oc[:], u8(T.q1[:, 0:64]), q1, grp="oy")
    for k in range(4):
        osd = dma("y" if k < 1 else "s", T.osc[4 * k:4 * k + 4, :], T.q1s[32 * k:32 * k + 4, 0:64], q1, grp="oy" if k < 1 else "os")
    for o in range(3):
        c = cp("v", T.ys1[:, 64 * o:64 * o + 64], T["ps%d" % (1 + o)][:, 0:64], my[o])
        dma("s" if o == 1 else "y", T.y[:, 192 * o + 128:192 * o + 192], T.ys1[:, 64 * o:64 * o + 64], c, grp="os" if o == 1 else "oy")
    op("y", None, oy)
    op("s", None, osd)
    op("g", None, og)
    _emit(ops, {"g": g, "v": V, "s": S, "p": P, "y": Y}, T)
